import numpy as np, ml_dtypes
CORES = [5,29,101,125,133,157,229,253]
N = 8
BF = ml_dtypes.bfloat16
W, C, H, CAP, RO = 2048, 512, 512, 32, 5
L = C >> 2
S16 = np.arange(16)
def owner(m):
    mb = np.zeros((8, W + 1), np.int32); mb[np.arange(8)[:, None, None], m] = np.arange(C)[None, :, None]
    return mb[:, :W]
def tight(m):
    return np.take_along_axis(m, np.argsort(m >= W, axis=-1, kind="stable"), -1)
def pick(a, j):
    return np.take_along_axis(a, j[:, :, None], 2)[:, :, 0]
def fill(n, order, s):
    s = np.minimum(s, 16 - n[order]); c = np.add.accumulate(s); left = W - np.add.reduce(n); n = n.copy()
    n[order] = n[order] + np.clip(left - (c - s), 0, s)
    return n
def sizes(rng):
    a = (W // C) * rng.choice(np.array([0.5, 1.0, 1.5]))
    n = fill(np.zeros(C, np.int64), rng.permutation(C), 1 + rng.poisson(a, C))
    return fill(n, rng.permutation(C), np.full(C, 16))
def seat(rng, n):
    m = np.full((C, 16), W, np.int64); m[S16 < n[:, None]] = rng.permutation(W)
    return m
def seats(rng):
    return np.stack([np.stack([seat(rng, sizes(rng)) for g in range(8)]) for q in range(N)])
def people(rng, m):
    typ = rng.integers(0, 16, (8, 24, 16)); own = np.take_along_axis(rng.integers(0, 24, (8, C)), owner(m), 1)
    ty = np.where(rng.random((8, W)) < rng.choice(np.array([0.3, 0.7, 0.95]), (8, 1)), own, rng.integers(0, 24, (8, W)))
    v = typ[np.arange(8)[:, None], ty]
    return np.clip(v + rng.integers(-3, 4, (8, W, 16)), 0, 15)
def wrap(x, a, m, li, w):
    def turn(v): return np.ascontiguousarray(v.transpose(0, 1, 3, 2)).reshape(N, 128, -1)
    return {"x0": turn(x).astype(np.float32).astype(BF), "ac": turn(a).astype(np.int32), "ml": turn(m).astype(np.int32),
            "lims": np.repeat(li, 16, axis=1).astype(np.int32), "wt": w.reshape(N, 128, 1).astype(np.int32)}
def setup_inputs(rng):
    m = seats(rng); x = np.stack([people(rng, b) for b in m])
    li = np.stack([rng.integers(30, 130, (N, 8)), rng.integers(20, 110, (N, 8))], axis=2)
    return wrap(x, rng.integers(0, W, (N, 8, H, 16)), m, li, rng.integers(0, 256, (N, 8, 16)))
def setup_inputs_ends(rng):
    ms, xs, as_, ls = [], [], [], []
    for q in range(N):
        m = []
        for g in range(8):
            n = np.zeros(C, np.int64); n[:4] = 16; n[C - 4:] = 16; o = 4 + rng.permutation(C - 8)
            n = fill(n, o, rng.choice(np.array([1, 1, 1, 16, 16, 8]), C - 8)); n = fill(n, o, np.full(C - 8, 16)); b = seat(rng, n)
            c = C - 4 + (g + q) % 4
            for v, k in ((0, 0), (W - 1, 15)):
                at = np.argwhere(b == v)[0]; b[at[0], at[1]] = b[c, k]; b[c, k] = v
            m.append(b)
        m = np.stack(m); ty = rng.integers(0, 5, (8, C, 1, 1)); ty[:, :4] = 4; ty[:, C - 4:] = 4
        edge = ((S16 != 2) & (S16 != 15))[None, None, :, None]
        val = np.where(ty == 0, True, np.where(ty == 1, False, np.where(ty == 2, rng.random((8, C, 16, 1)) < 0.5, np.where(ty == 3, rng.random((8, C, 16, 16)) < 0.5, edge))))
        x = np.zeros((8, W + 1, 16), np.int64); x[np.arange(8)[:, None, None], m] = 15 * val
        far = rng.random((8, H, 16)) < np.where(rng.random((8, H, 1)) < 0.4, 1.1, 0.55)
        ms.append(m); xs.append(x[:, :W]); as_.append(np.where(far, (W - 1) * rng.integers(0, 2, (8, H, 16)), rng.integers(0, W, (8, H, 16))))
        ls.append(np.array([[0, 0], [0, 240], [240, 0], [240, 240]])[(np.arange(8) // 2 + q) % 4])
    w = 255 * rng.integers(0, 2, (N, 8, 16)); w[:, 3::4] = 255; w[:, 1] = 0
    return wrap(np.stack(xs), np.stack(as_), np.stack(ms), np.stack(ls), w)
def setup_inputs_corners(rng):
    ms, xs, as_, ls = [], [], [], []
    for q in range(N):
        m = []; l = []; x = rng.integers(0, 16, (8, W, 16))
        for g in range(8):
            k = (g + q) & 7; n = np.zeros(C, np.int64); o = rng.permutation(C); z = 4 * rng.permutation(L); u = o[(o & 3) != 0]
            if k < 2:
                n[z[:CAP + k]] = 16; n = fill(n, u, rng.choice(np.array([1, 4, 8, 16]), len(u))); n = fill(n, u, np.full(len(u), 16))
            elif k == 2: n[:] = W // C
            elif k == 3:
                n[:] = W // C; n[o[:3]] = 0; n[o[3:6]] = 2 * (W // C)
            elif k == 4:
                n[z[:L // 2]] = 8; n = fill(n, u, rng.choice(np.array([8, 9]), len(u)))
            elif k == 5: n = fill(n, o, np.full(C, 16))
            elif k == 6:
                n[z] = 1; n = fill(n, u, rng.choice(np.array([15, 16]), len(u)))
            else:
                n = sizes(rng); x[g] = rng.integers(0, 2, (W, 16))
            m.append(seat(rng, n)); l.append(((0, 240), (0, 240), (240, 0), (0, 0), (240, 240), (240, 0), (240, 0), (int(rng.integers(2, 14)), int(rng.integers(2, 9))))[k])
        m = np.stack(m); mb = owner(m); mode = rng.integers(0, 6, (8, H, 1)); a = rng.integers(0, W, (8, H, 16)); zero = []
        for g in range(8):
            c0 = np.nonzero((mb[g] & 3) == 0)[0]
            if len(c0) == 0: c0 = np.arange(W)
            zero.append(c0[rng.integers(0, len(c0), (H, 16))])
        a = np.where(mode == 1, a[:, :, :1], np.where(mode == 2, (W - 1) * rng.integers(0, 2, (8, H, 16)), np.where(mode == 3, np.arange(H)[None, :, None] + H * rng.integers(0, W // H, (8, H, 16)),
            np.where(mode == 4, np.stack(zero), np.where(mode == 5, a[:, :, S16 & 1], a)))))
        ms.append(m); xs.append(x); as_.append(a); ls.append(np.array(l))
    w = np.where(rng.random((N, 8, 16)) < 0.5, rng.integers(0, 256, (N, 8, 16)), rng.choice(np.array([0, 1, 255]), (N, 8, 16)))
    return wrap(np.stack(xs), np.stack(as_), np.stack(ms), np.stack(ls), w)
def setup_inputs_brim(rng):
    ms, xs, as_, ls = [], [], [], []
    for q in range(N):
        m = []; l = []; x = rng.integers(0, 16, (8, W, 16)); a = rng.integers(0, W, (8, H, 16))
        for g in range(8):
            k = (g + q) & 3; n = np.zeros(C, np.int64); o = rng.permutation(C); z = 4 * rng.permutation(L); u = o[(o & 3) != 0][:L]
            if k == 1:
                n[z] = 1; n[u] = 2; n = fill(n, o, rng.choice(np.array([0, 2, 4, 6]), C)); n = fill(n, o, 8 - n[o])
            else:
                n[z] = 4; n = fill(n, rng.permutation(np.concatenate([z, u])), rng.choice(np.array([0, 1, 4, 8, 12]), 2 * L)); n = fill(n, rng.permutation(z), np.full(L, 12))
            b = seat(rng, n)
            if k == 1:
                old = b[z, rng.integers(0, n[z])]; h = rng.permutation(H)[:L]; new = h + H * rng.integers(0, W // H, L); p = np.full(W + 1, W)
                p[old] = new; p[np.setdiff1d(np.arange(W), old)] = rng.permutation(np.setdiff1d(np.arange(W), new)); b = p[b]
                x[g] = rng.integers(1, 16, (W, 16)); x[g, new] = 0
                x[g, b[u, 0]] = np.where(S16 == rng.integers(0, 16, (L, 1)), 0, 12); x[g, b[u, 1]] = np.where(S16 == rng.integers(0, 16, (L, 1)), 1, 12)
                a[g, h] = np.where((rng.random((L, 16)) < 0.25) & (S16 > 1), new[rng.integers(0, L, (L, 16))], np.where((S16 & 1) == 1, b[u, 0][:, None], b[np.roll(u, -1), 1][:, None]))
            elif k == 2:
                p = np.argsort(rng.random((L, 16)), axis=1); j = np.argsort(rng.random((L, 4)), axis=1); x[g] = rng.integers(1, 10, (W, 16))
                x[g, b[z, j[:, 0]]] = 0; x[g, b[z, j[:, 1]]] = np.where(p < 10, 15, np.where(p == 10, 1, 0)); x[g, b[z, j[:, 2]]] = np.where(p >= 6, 15, np.where(p < 2, 1, 0))
            elif k == 3:
                ty = rng.integers(0, 3, (W, 1)); x[g] = np.where(ty == 0, 15, np.where((ty == 1) & (S16 == rng.integers(0, 16, (W, 1))), 1, 0))
            m.append(b); l.append(((0, 0), (240, 0), (0, 0), (0, 239 + (g >> 2)))[k])
        ms.append(np.stack(m)); xs.append(x); as_.append(a); ls.append(np.array(l))
    return wrap(np.stack(xs), np.stack(as_), np.stack(ms), np.stack(ls), rng.integers(0, 256, (N, 8, 16)))
def setup_inputs_ties(rng):
    m = seats(rng); two = np.array([[0, 1], [7, 8], [0, 15], [3, 6]])[(np.arange(8)[None, :] + np.arange(N)[:, None]) & 3]
    pool = rng.integers(0, 2, (N, 8, 12, 16)); pool = np.where(pool == 1, two[:, :, None, 1:], two[:, :, None, :1])
    kind = rng.integers(0, 12, (N, 8, W)); x = pool[np.arange(N)[:, None, None], np.arange(8)[None, :, None], kind]
    step = two[:, :, 1] - two[:, :, 0]; li = np.stack([step * rng.integers(5, 14, (N, 8)), step * rng.integers(3, 11, (N, 8))], axis=2)
    known = rng.integers(0, W, (N, 8, 40)); k = rng.integers(0, 40, (N, 8, H * 16))
    a = np.where(rng.random((N, 8, H, 1)) < 0.5, np.take_along_axis(known, k, 2).reshape(N, 8, H, 16), rng.integers(0, W, (N, 8, H, 16)))
    return wrap(x, a, m, np.minimum(li, 240), rng.integers(0, 256, (N, 8, 16)))
def setup_inputs_spread(rng):
    x = rng.integers(0, 2 ** rng.integers(0, 5, (N, 8, W, 1)), (N, 8, W, 16)); m = []
    for q in range(N):
        for g in range(8):
            n = fill(np.zeros(C, np.int64), rng.permutation(C), rng.choice(np.array([0, 1, 1, 2, 3, 5, 16]), C)); m.append(seat(rng, fill(n, rng.permutation(C), np.full(C, 16))))
    a = np.minimum((W * rng.random((N, 8, H, 16)) ** 3).astype(np.int64), W - 1); w = np.minimum((np.exp2(8 * rng.random((N, 8, 16))) - 1).astype(np.int64), 255)
    return wrap(x, a, np.stack(m).reshape(N, 8, C, 16), rng.integers(0, 241, (N, 8, 2)), w)
def check_inputs(d):
    bad = []
    for k, lo, hi in (("x0", 0, 15), ("ac", 0, W - 1), ("ml", 0, W), ("lims", 0, 240), ("wt", 0, 255)):
        a = np.asarray(d[k]).astype(np.float64)
        if not (np.min(a) >= lo and np.max(a) <= hi): bad.append("range of " + k)
    a = np.asarray(d["x0"]).astype(np.float64)
    if np.any(a != np.floor(a)): bad.append("whole numbers in x0")
    m = np.asarray(d["ml"]).astype(np.int64).reshape(N, 8, 16, C)
    if np.any(np.sort(m.reshape(N, 8, 16 * C), axis=-1) != np.minimum(np.arange(16 * C), W)): bad.append("every agent once in ml")
    if np.any((m[:, :, 1:] < W) & (m[:, :, :-1] >= W)): bad.append("members before empty slots in ml")
    l = np.asarray(d["lims"]).reshape(N, 8, 16, 2)
    if np.any(l != l[:, :, :1]): bad.append("lims alike in a group")
    return bad
def reference(x0, ac, ml, lims, wt):
    X = np.zeros((N, 8, W + 1, 16), np.int32)
    X[:, :, :W] = x0.astype(np.float32).astype(np.int32).reshape(N, 8, 16, W).transpose(0, 1, 3, 2)
    A = ac.reshape(N, 8, 16, H).transpose(0, 1, 3, 2); M = np.array(ml.reshape(N, 8, 16, C).transpose(0, 1, 3, 2))
    lim = lims.reshape(N, 8, 16, 2)[:, :, 0].astype(np.int64); wv = wt.reshape(N, 8, 16).astype(np.int64)
    G = np.arange(8)[:, None]; G3 = G[:, :, None]; low = np.tri(L, L, -1, dtype=bool); z = np.zeros(N, np.int64)
    for t in range(RO):
        cl = t & 3; lane = 4 * np.arange(L) + cl; M2 = M.copy(); X2 = X.copy(); z2 = np.zeros(N, np.int64); go = []
        for r in range(N):
            x, m, mb = X[r], M[r], owner(M[r])
            own = m[:, lane]; here = own < W; live = here[:, :, 0]; tx = x[G3, own]; U = np.max(tx, axis=2)
            gr = np.where(here, np.sum(U[:, :, None] - tx, axis=3), -1); s = pick(own, np.argmax(gr, axis=2)); xs = x[G, s]
            ds = np.where(here, np.sum((tx - xs[:, :, None]) ** 2, axis=3), -1)
            an = A[r][G, s & (H - 1)]; ad = mb[G3, an]; fit = live[:, :, None] & ((ad & 3) != cl); has = np.any(fit, axis=2)
            d = pick(ad, np.argmin(np.where(fit, np.sum((x[G3, an] - xs[:, :, None]) ** 2, axis=3), 2 ** 20), axis=2))
            first = ~np.any((d[:, :, None] == d[:, None, :]) & has[:, None, :] & low, axis=2)
            dm = m[G, d]; dh = dm < W; td = x[G3, dm]; V = np.maximum(U, np.max(td, axis=2))[:, :, None]
            worst = np.maximum(np.max(np.where(here, np.sum(V - tx, axis=3), 0), axis=2), np.max(np.where(dh, np.sum(V - td, axis=3), 0), axis=2))
            mer = has & first & (np.sum(here, axis=2) + np.sum(dh, axis=2) <= 16) & (worst <= lim[r, :, :1] + (z[r] & 15))
            want = live & ~mer & (np.max(gr, axis=2) > lim[r, :, 1:])
            xg = x[G, pick(own, np.argmax(ds, axis=2))]; away = here & (np.sum((tx - xg[:, :, None]) ** 2, axis=3) < ds)
            vacant = m[:, :, 0] >= W; free = np.argsort(~vacant, axis=1, kind="stable")
            k = np.add.accumulate(want.astype(np.int64), axis=1) - want.astype(np.int64)
            spl = want & (k < np.sum(vacant, axis=1)[:, None]); e = np.take_along_axis(free, k, 1)
            both = tight(np.concatenate([own, dm], axis=2))[:, :, :16]
            M2[r][:, lane] = np.where(mer[:, :, None], both, np.where(spl[:, :, None], tight(np.where(away, W, own)), own))
            a, b = np.nonzero(mer); M2[r][a, d[a, b]] = W
            a, b = np.nonzero(spl); M2[r][a, e[a, b]] = tight(np.where(away, own, W))[a, b]
            idle = live & ~mer & ~spl; a, b = np.nonzero(idle & (np.add.accumulate(idle.astype(np.int64), axis=1) <= CAP))
            go.append((a, s[a, b], xs[a, b])); z2[r] = np.sum(mer)
        for r in range(N):
            q = (r + 1 + t % (N - 1)) % N; a, sa, xa = go[r]
            v = np.sum(wv[q][a] * xa, axis=1) & (W - 1); mm = M2[q][a, owner(M2[q])[a, v]]; y = X[q][a[:, None], mm]
            j = np.argmin(np.where(mm < W, np.sum((y - xa[:, None]) ** 2, axis=2), 2 ** 20), axis=1)
            X2[r][a, sa] = (xa + y[np.arange(len(a)), j]) >> 1
        X, M, z = X2, M2, z2
    return {"ym": np.ascontiguousarray(M.transpose(0, 1, 3, 2)).reshape(N, 128, C).astype(np.float32),
            "yx": np.ascontiguousarray(X[:, :, :W].transpose(0, 1, 3, 2)).reshape(N, 128, W).astype(np.float32).astype(BF)}

@@ -1,0 +1,763 @@
+from concourse.mybir import dt, AluOpType as A, AxisListType as AX_, ActivationFunctionType as F
+
+RO, CA = 5, 256
+CB = 512 - CA
+NA, NB = 16 * CA, 16 * CB
+BIG = 1.0e9
+S, B, H, I, U = "float32", "bfloat16", "float16", "int32", "uint16"
+
+SCRATCH = {}
+
+
+def _sb(names, cols, dtype):
+    for n in names.split():
+        SCRATCH[n] = ("sbuf", [128, cols], dtype)
+
+
+_sb("X", 2304, B)
+_sb("AC4", 2064, I)
+_sb("MI", 512, I)
+_sb("LI", 2, I)
+_sb("WI", 1, I)
+_sb("W", 664, S)
+_sb("OT", 2064 + NA, S)
+_sb("OB", 2064 + NB, B)
+_sb("VE", max(NA, 2048), S)
+_sb("ZE", max(NA, 2048), B)
+_sb("VB", NB, B)
+_sb("ZB", NB, B)
+_sb("V0 Jf J2f t512a t512b t512c", 512, S)
+_sb("J3", 512, I)
+_sb("MS", max(NA, 2048), B)
+_sb("MIN", 128, B)
+_sb("FM", 1024, B)
+_sb("T US Z REP SQ AX OG DT", 2048, B)
+_sb("DS", 2176, S)
+_sb("OWN AN DM CREP MVO", 128, U)
+_sb("INO", 512, U)
+_sb("OWNH DMH DSE R16 ID16 ID16x NID16 TRI D1R PD KB KV SEL5 SR PS MR MP WR SPR SPP IR VR VP NVP KP RP EVH Q1 Q2 "
+    "A1 A2 A3 MD NR NP BR BP XP", 128, H)
+_sb("ZS ZD ZN ZBB ZM ZW ZSP ZI ZV ZQ QR8 QP", 128, H)
+_sb("EO ED IDB NIDB BD NBD BT IDE NIDE ID1K CK CKP KA DEAD HWB WTB ONEB Vv WV XB SQS SQB NV", 128, B)
+_sb("ONE16", 128, H)
+_sb("Y", 144, B)
+_sb("S1 S2 S3 SB W16L WL PW2 lv mb L1 cl SM q1a q2a STM EV ELS DUM f128a f128b VFP QPF QSC", 128, S)
+_sb("Pa Pb Mi Aa", 264, I)
+_sb("STI", 256, I)
+_sb("DG", 1024, H)
+_sb("AB ABS", 1024, B)
+_sb("SH", 2048, B)
+_sb("PIi", 4, I)
+_sb("PC", 32, S)
+_sb("J", 512, I)
+_sb("J4 J15", 128, I)
+_sb("blk16 blk128 blkN blkI blk32 blkm blk2k CI C528", 8, H)
+_sb("blkf", 8, S)
+_sb("C640 w32k w8k w2k w512 w1 w2 og0 og1 og2 og3 SEL0", 8, B)
+_sb("k8 sv8 sx8 b8 bb8 a8 d8 q8 qq8", 8, I)
+_sb("lim8 lim28 thr8 live8 gr8 wp8 has8 dp8 nD d18 mn8 tm8 f8 sz8 P0 c8 sp8 ms8 v8 nf8 nfs8", 8, S)
+_sb("S16 B16 D16 N16 K16 TG16 RT16 XT16", 8, U)
+_sb("NFH", 8, H)
+_sb("VC", 512, B)
+_sb("VTb", 32, B)
+_sb("CSs CVp rk", 32, S)
+_sb("CVn", 32, H)
+_sb("F16", 32, U)
+_sb("FREE", 1168, S)
+_sb("mc", 4, S)
+_sb("mci", 4, I)
+_sb("RESW", 160, I)
+_sb("HO EH", 32, B)
+_sb("HL", 32, U)
+_sb("VI VI2", 2, I)
+_sb("VV16 H16 J16", 2, U)
+_sb("QZ QRp QD QS", 512, B)
+_sb("hs", 32, S)
+_sb("YM", 512, S)
+for _t in range(RO):
+    _sb("XV%d" % _t, 160, B)
+    _sb("QI%d" % _t, 32, B)
+    _sb("SN%d RS%d" % (_t, _t), 32, I)
+_ARENA = {}
+
+
+def _pack():
+    keep, pos = {}, {}
+    big = ("X", "T", "W", "XV", "QI", "SN", "RS")
+    for n, (w, sh, d) in SCRATCH.items():
+        if n in ("X", "T", "W", "AC4", "OT", "OB", "FREE", "RESW", "DS", "QD", "WV") or n[:2] in ("XV", "QI", "SN", "RS"):
+            keep[n] = (w, sh, d)
+            _ARENA[n] = (n, 0, sh[1], d)
+        else:
+            c = -(-sh[1] // 16) * 16
+            o = pos.get(d, 0)
+            _ARENA[n] = ("ar_" + d, o, sh[1], d)
+            pos[d] = o + c
+    for d in pos:
+        keep["ar_" + d] = ("sbuf", [128, pos[d]], d)
+    return keep
+
+
+SCRATCH = _pack()
+for _k in range(8):
+    SCRATCH["p%d" % _k] = ("psum", [128, 512], S)
+    _ARENA["p%d" % _k] = ("p%d" % _k, 0, 512, S)
+SEMAPHORES = ["v", "p", "s", "k"] + ["ld%d" % i for i in range(8)] + ["st0", "st1"]
+for _t in range(RO):
+    SEMAPHORES += ["rq%d" % _t, "rs%d" % _t, "lq%d" % _t, "ls%d" % _t, "fq%d" % _t, "fs%d" % _t, "mq%d" % _t, "ms%d" % _t]
+
+
+def _mask(topo, a, b):
+    es = topo.engines(a, b)[:8]
+    return sum(1 << e for e in es), len(es)
+
+
+def _relay(topo, a, b, which):
+    if topo.may_write(a, b):
+        return None
+    c = [h for h in topo.cores_of(a) if h != a and topo.may_write(h, b)]
+    c.sort(key=lambda h: (topo.die(h) != topo.die(a), h))
+    return c[which % len(c)]
+
+
+def _relay_program(g, core, T, topo):
+    used = []
+    for t in range(RO):
+        for r in range(8):
+            a, b = T.cores[r], T.cores[(r + 1 + t % 7) % 8]
+            for (x, y, buf, arr, fwd, loc, which) in ((a, b, "QI", "rq", "fq", "mq", 0), (b, a, "RS", "rs", "fs", "ms", 1)):
+                if _relay(topo, x, y, which) == core:
+                    _, n = _mask(topo, x, core)
+                    m, n2 = _mask(topo, core, y)
+                    rid, pid = topo.addr(y, core)
+                    g.wait_ge(T.sem["%s%d" % (fwd, t)], n)
+                    g.remote_dma(T["%s%d" % (buf, t)][:], T["%s%d" % (buf, t)][:], T.sem["%s%d" % (arr, t)],
+                                 T.sem["%s%d" % (loc, t)], pid, rid, m)
+                    used.append((T.sem["%s%d" % (loc, t)], n2))
+    for s, n in used:
+        g.wait_ge(s, n)
+
+
+def rank_program(g, core, T, topo):
+    rank = T.rank_of(core)
+    if rank is None:
+        _relay_program(g, core, T, topo)
+        return
+    E = {"v": g.vector, "p": g.tensor, "s": g.scalar, "k": g, "y": g.sync}
+    cnt = {"v": 0, "p": 0, "s": 0, "k": 0}
+    known = {e: {} for e in E}
+    snap = {}
+    log = {}
+    total = {}
+
+    def u(name, lo=0, hi=None, st=1, p=None):
+        buf, o, n, _d = _ARENA[name]
+        hi = n if hi is None else hi
+        a, b = o + lo, o + hi
+        rows = slice(None) if p is None else slice(p[0], p[1])
+        t = T[buf]
+        ap = t[rows, a:b:st] if st != 1 else t[rows, a:b]
+        return (ap, [(buf, a, b)])
+
+    def ix(win, off):
+        return (win[0].indirect(off[0]), win[1] + off[1])
+
+    def need(e, reads, writes):
+        w = {}
+
+        def add(sem, val):
+            if w.get(sem, 0) < val:
+                w[sem] = val
+        for kind, lst in ((0, reads), (1, writes)):
+            for (b, lo, hi) in lst:
+                psum = len(b) == 2 and b[0] == "p"
+                for (l2, h2, e2, sem, val, wr) in log.get(b, ()):
+                    if psum:
+                        if e2 == e:
+                            if not (wr and e != "p") or (kind == 1 and not wr) or not (lo < h2 and l2 < hi):
+                                continue
+                        add(sem, val)
+                    elif lo < h2 and l2 < hi and (kind or wr):
+                        if e2 == e and e in ("v", "s", "p") and not wr:
+                            continue
+                        add(sem, val)
+        return w
+
+    def wait(e, w):
+        for sem in w:
+            if known[e].get(sem, 0) < w[sem]:
+                E[e].wait_ge(T.sem[sem], w[sem])
+                known[e][sem] = w[sem]
+                for s2, v2 in snap.get((sem, w[sem]), {}).items():
+                    if known[e].get(s2, 0) < v2:
+                        known[e][s2] = v2
+
+    def note(e, reads, writes, sem, val):
+        d = dict(known[e])
+        d[sem] = max(d.get(sem, 0), val)
+        snap[(sem, val)] = d
+        total[sem] = val
+        for (b, lo, hi) in writes:
+            old = log.get(b, [])
+            log[b] = [x for x in old if not (lo <= x[0] and x[1] <= hi)] + [(lo, hi, e, sem, val, True)]
+        for (b, lo, hi) in reads:
+            old = log.get(b, [])
+            log[b] = [x for x in old if not (x[2] == e and not x[5] and lo <= x[0] and x[1] <= hi and x[3] == sem)] + [(lo, hi, e, sem, val, False)]
+
+    def op(e, fn, outs, ins, dma=None):
+        rd = [r for x in ins for r in x[1]]
+        wr = [r for x in outs for r in x[1]]
+        wait(e, need(e, rd, wr))
+        i = fn()
+        if dma:
+            i.then_inc(T.sem[dma], 16)
+            note(e, rd, wr, dma, 16)
+        else:
+            cnt[e] += 1
+            i.then_inc(T.sem[e], 1)
+            note(e, rd, wr, e, cnt[e])
+
+    def _c(x):
+        return x[0] if isinstance(x, tuple) else x
+
+    def _r(*xs):
+        return [x for x in xs if isinstance(x, tuple)]
+
+    v, sc = g.vector, g.scalar
+
+    def cp(o, i, scatter=None):
+        op("v", lambda: v.tensor_copy(o[0], i[0]), [o], [i] + (scatter or []))
+
+    def ts(o, i, s1, o1, s2=None, o2=None):
+        if o2 is None:
+            op("v", lambda: v.tensor_scalar(o[0], i[0], _c(s1), None, o1), [o], [i] + _r(s1))
+        else:
+            op("v", lambda: v.tensor_scalar(o[0], i[0], _c(s1), _c(s2), o1, o2), [o], [i] + _r(s1, s2))
+
+    def tt(o, a, b, o1):
+        op("v", lambda: v.tensor_tensor(o[0], a[0], b[0], o1), [o], [a, b])
+
+    def scan(o, a, b, o1, o2):
+        op("v", lambda: v.tensor_tensor_scan(o[0], a[0], b[0], 0.0, o1, o2), [o], [a, b])
+
+    def fill(o, c):
+        op("v", lambda: v.memset(o[0], c), [o], [])
+
+    def act(o, i, f, scale=None, bias=None):
+        kw = {}
+        if scale is not None:
+            kw["scale"] = _c(scale)
+        if bias is not None:
+            kw["bias"] = _c(bias)
+        op("s", lambda: sc.activation(o[0], i[0], f, **kw), [o], [i] + _r(scale, bias))
+
+    def mm(items):
+        rd = [r for x in items for y in x[1:] for r in y[1]]
+        wr = [r for x in items for r in x[0][1]]
+        wait("p", need("p", rd, wr))
+        n = len(items)
+        for j, (o, a, b) in enumerate(items):
+            i = g.tensor.matmul(o[0], a[0], b[0], j == 0, j == n - 1)
+        cnt["p"] += 1
+        i.then_inc(T.sem.p, 1)
+        note("p", rd, wr, "p", cnt["p"])
+
+    def dma(e, o, i, sem):
+        op(e, lambda: E[e].dma_start(o[0], i[0]), [o], [i], dma=sem)
+
+    def ext(ap, name):
+        return (ap, [(name, 0, 1)])
+
+    def arrived(e, name, sem, n):
+        if known[e].get(sem, 0) < n:
+            E[e].wait_ge(T.sem[sem], n)
+            known[e][sem] = n
+        total[sem] = n
+
+    def send(dst, buf_src, buf_dst, sem, fwd, loc, which):
+        to = _relay(topo, core, dst, which)
+        d = dst if to is None else to
+        m, n = _mask(topo, core, d)
+        rid, pid = topo.addr(d, core)
+        name = _ARENA[buf_src][0]
+        wait("k", need("k", [(name, 0, 32)], []))
+        g.remote_dma(T[buf_dst][:], T[buf_src][:, 0:32], T.sem[sem if to is None else fwd], T.sem[loc], pid, rid, m)
+        total[loc] = n
+
+    def landed_n(src, which):
+        via = _relay(topo, src, core, which)
+        return _mask(topo, src if via is None else via, core)[1]
+
+    def hold(o, z):
+        scan(o, u("MS", 0, 128), z, A.mult, A.add)
+
+    def k16(name, k, n=128, p=None):
+        return u(name, k, n, 16, p)
+
+    def sums(ps, base, src, w, p=None):
+        return [(u(ps, base + k, base + 128, 16, p), u(src, k, None, 16), u(w)) for k in range(16)]
+
+    fill(u("X", 0, 16), 0.0)
+    fill(u("X", 2048, 2304), 0.0)
+    fill(u("AC4", 0, 8), 0)
+    dma("y", u("MI"), ext(T.ml[:], "in_ml"), "ld0")
+    op("k", lambda: g.iota(u("PIi", 0, 1)[0], [[0, 1]], 0, 1), [u("PIi", 0, 1)], [])
+    op("k", lambda: g.iota(u("J")[0], [[1, 512]], 0, 0), [u("J")], [])
+    dma("s", u("X", 1, 2049), ext(T.x0[:], "in_x"), "ld1")
+    dma("y", u("LI"), ext(T.lims[:], "in_l"), "ld2")
+    dma("s", u("WI"), ext(T.wt[:], "in_w"), "ld3")
+    for q in range(4):
+        dma("y", u("AC4", 1 + 512 * q, 513 + 512 * q), ext(T.ac[:], "in_a"), "ld%d" % (4 + q))
+    op("k", lambda: g.iota(u("J2f")[0], [[1, 128], [0, 4]], 0, 0, allow_small_or_imprecise_dtypes=True), [u("J2f")], [])
+    op("k", lambda: g.iota(u("J3")[0], [[0, 128], [1, 4]], 0, 0), [u("J3")], [])
+    op("k", lambda: g.iota(u("Jf")[0], [[1, 512]], 1, 0, allow_small_or_imprecise_dtypes=True), [u("Jf")], [])
+    op("k", lambda: g.iota(u("OT", 0, 2064)[0], [[0, 2064]], 0, 0, allow_small_or_imprecise_dtypes=True), [u("OT", 0, 2064)], [])
+    op("k", lambda: g.iota(u("OB", 0, 2064)[0], [[0, 2064]], 0, 0, allow_small_or_imprecise_dtypes=True), [u("OB", 0, 2064)], [])
+
+    fill(u("MS"), 1.0)
+    fill(u("MS", 0, None, 16), 0.0)
+    fill(u("ZE"), 0.0)
+    fill(u("ZB"), 0.0)
+    fill(u("MIN"), -BIG)
+    fill(u("MIN", 0, None, 16), BIG)
+    fill(u("W"), 0.0)
+    J, J4, J15 = u("J", 0, 128), u("J4"), u("J15")
+
+    def col(n):
+        return u("PC", n, n + 1)
+    P, P4, P15 = col(0), col(1), col(2)
+    ts(u("PIi", 1, 2), u("PIi", 0, 1), 4, A.logical_shift_right)
+    ts(u("PIi", 2, 3), u("PIi", 0, 1), 15, A.bitwise_and)
+    cp(u("PC", 0, 3), u("PIi", 0, 3))
+    ts(J4, J, 4, A.logical_shift_right)
+    ts(J15, J, 15, A.bitwise_and)
+    ts(col(3), P15, 4, A.is_equal)
+    ts(col(4), P15, 4, A.is_equal, 128.0, A.mult)
+    ts(col(5), P15, 5, A.is_equal)
+    act(u("t512a"), u("J2f"), F.Identity, scale=col(3), bias=col(4))
+    act(u("t512b"), u("Jf"), F.Copy, scale=col(5))
+    ts(u("t512c"), u("J3"), P15, A.is_equal, 64.0, A.mult)
+    tt(u("t512a"), u("t512a"), u("t512b"), A.add)
+    tt(u("V0"), u("t512a"), u("t512c"), A.add)
+    cp(u("ZE", 0, NA, 16), u("V0", 0, CA))
+    cp(u("ZB", 0, NB, 16), u("V0", CA, 512))
+    scan(u("VE", 0, NA), u("MS", 0, NA), u("ZE", 0, NA), A.mult, A.add)
+    ts(u("t512b"), u("MI"), 2048, A.is_lt)
+    ts(u("t512c"), u("MI"), 1, A.add)
+    tt(u("W", 1, 513), u("t512b"), u("t512c"), A.mult)
+    ts(col(6), P15, 2064, A.add)
+    ts(u("DUM"), J, 16, A.mult, col(6), A.add)
+    ts(u("t512a", 0, CA), u("J", 0, CA), 16, A.mult, col(6), A.add)
+    ts(u("t512a", CA, 512), u("J", 0, CB), 16, A.mult, col(6), A.add)
+    ts(u("t512b"), u("MI"), 2048, A.is_equal)
+    tt(u("t512b"), u("t512b"), u("t512a"), A.mult)
+    tt(u("t512b"), u("t512b"), u("W", 1, 513), A.add)
+    cp(u("INO"), u("t512b"))
+    act(ix(u("OT"), u("INO", 0, CA)), u("VE", 0, NA), F.Silu)
+
+    ts(u("IDB"), J, P, A.is_equal)
+    ts(u("NIDB"), J, P, A.is_equal, -1.0, A.mult)
+    ts(u("ID16"), J, P, A.is_equal)
+    ts(u("NID16"), J, P, A.is_equal, -1.0, A.mult)
+    ts(u("ID16x"), J, P, A.is_equal, 16.0, A.mult)
+    ts(u("IDE"), J, P, A.is_equal, 2.0 ** 23, A.mult)
+    ts(u("NIDE"), J, P, A.is_equal, -2.0 ** 23, A.mult)
+    ts(u("ID1K"), J, P, A.is_equal, 1024.0, A.mult)
+    ts(u("BD"), J4, P4, A.is_equal)
+    ts(u("NBD"), J4, P4, A.is_equal, -1.0, A.mult)
+    ts(u("R16"), J15, P15, A.is_equal)
+    ts(u("CK"), J15, 2048.0, A.mult)
+    ts(u("CKP"), J15, 1.0, A.add)
+    ts(u("blk16"), u("J", 0, 8), P4, A.is_equal)
+    ts(u("blkf"), u("J", 0, 8), P4, A.is_equal)
+    ts(u("w32k"), u("BD", 0, None, 16), 32768.0, A.mult)
+    ts(u("w8k"), u("BD", 0, None, 16), 8192.0, A.mult)
+    ts(u("w2k"), u("BD", 0, None, 16), 2048.0, A.mult)
+    ts(u("w512"), u("BD", 0, None, 16), 512.0, A.mult)
+    ts(u("w1"), u("BD", 0, None, 16), 1.0, A.mult)
+    ts(u("w2"), u("BD", 0, None, 16), 2.0, A.mult)
+    fill(u("Z"), 0.0)
+    for z in "ZS ZD ZN ZBB ZM ZW ZSP ZI ZV ZQ".split():
+        ts(u(z), J, 0.0, A.mult)
+
+    def late_constants():
+        ts(col(7), P, -16.0, A.mult, 2047.0, A.add)
+        ts(u("KB"), J15, -1.0, A.mult, col(7), A.add)
+        ts(col(8), P, 16.0, A.mult)
+        ts(u("KV"), J15, col(8), A.add)
+        cp(u("CREP"), J)
+        ts(col(9), P, 0.0, A.is_equal, 512.0, A.mult)
+        ts(col(10), P, 1.0, A.is_equal, -2.0 ** 24, A.mult)
+        ts(u("KA"), J15, col(9), A.mult, col(10), A.add)
+        fill(u("ONEB"), 1.0)
+        cp(u("ONE16"), u("ONEB"))
+        ts(col(11), P15, 0.0, A.is_equal, 2.0 ** 25, A.mult)
+        ts(u("DEAD"), u("BD"), col(11), A.mult)
+        ts(col(12), P15, 4.0, A.is_lt, 1.0 / 64, A.mult)
+        tt(col(12), col(12), P15, A.mult)
+        ts(col(13), P15, 4.0, A.is_equal, 4.0, A.mult)
+        tt(col(12), col(12), col(13), A.add)
+        ts(u("HWB"), u("BD"), col(12), A.mult)
+        for c in range(4):
+            ts(col(14), P15, float(c), A.is_equal, 2.0 ** 19, A.mult)
+            tt(col(15), col(14), col(12), A.add)
+            ts(u("og%d" % c), u("BD", 0, None, 16), col(15), A.mult)
+        ts(u("TRI"), J, P, A.is_gt)
+        fill(u("FM"), -4096.0)
+        fill(u("FM", 0, None, 128), 4096.0)
+        ts(u("blk128"), u("J", 0, 8), P4, A.is_equal, 128.0, A.mult)
+        ts(col(16), P, -1.0, A.mult, -528.0, A.add)
+        ts(u("blkN"), u("J", 0, 8), P4, A.is_equal, col(16), A.mult)
+        ts(col(17), P, 16.0, A.add)
+        ts(u("blkI"), u("J", 0, 8), P4, A.is_equal, col(17), A.mult)
+        ts(col(18), P, 32.0, A.add)
+        ts(u("blk32"), u("J", 0, 8), P4, A.is_equal, col(18), A.mult)
+        ts(u("blkm"), u("J", 0, 8), P4, A.is_equal, -640.0, A.mult)
+        ts(u("blk2k"), u("J", 0, 8), P4, A.is_equal, 2048.0, A.mult)
+        fill(u("C640"), 640.0)
+        ts(u("CI"), u("J", 0, 8), 16.0, A.mult, P15, A.add)
+        ts(col(19), P15, 528.0, A.add)
+        ts(u("C528"), u("J", 0, 8), 16.0, A.mult, col(19), A.add)
+        ts(u("SEL5"), u("BD"), col(5), A.mult)
+        ts(u("BT"), J, P, A.is_le, -1.0, A.mult)
+        tt(u("BT"), u("BT"), u("BD"), A.mult)
+        ts(col(20), P, 15.0, A.add)
+        ts(col(21), P15, 0.0, A.is_equal)
+        ts(u("Y"), u("J", 0, 144), col(20), A.is_equal, col(21), A.mult)
+        ts(u("SEL0"), u("BD", 0, None, 16), col(21), A.mult)
+        ts(col(22), P15, 656.0, A.add)
+        ts(u("CVp"), u("J", 0, 32), 16.0, A.mult, col(22), A.add)
+        ts(u("CVn"), u("CVp"), -1.0, A.mult)
+        fill(u("FREE"), 0.0)
+        fill(u("DS", 2048, 2176), 0.0)
+        fill(u("RESW"), 0)
+        fill(u("QZ"), 0.0)
+        fill(u("Aa"), 0)
+        for t in range(RO):
+            fill(u("XV%d" % t), 0.0)
+        for s in range(16):
+            o, i = u("SH", 128 * s, 128 * s + 128), u("BD")
+            op("k", lambda: g.affine_select(o[0], i[0], [[1, 128]], A.is_equal, 0.0, -s, -1), [o], [i])
+        cp(u("PC", 24, 26), u("LI"))
+        cp(u("PC", 26, 27), u("WI"))
+        ts(u("WTB"), u("BD"), col(26), A.mult)
+        ts(u("NFH"), u("SEL0"), col(24), A.mult)
+        mm([(u("p6", 0, 8), u("ONE16"), u("NFH"))])
+        cp(u("lim8"), u("p6", 0, 8))
+        cp(u("thr8"), u("p6", 0, 8))
+        ts(u("NFH"), u("SEL0"), col(25), A.mult)
+        mm([(u("p6", 0, 8), u("ONE16"), u("NFH"))])
+        cp(u("lim28"), u("p6", 0, 8))
+
+    def tile(src_rep, prod, blk, out, extra=(), ps="p6"):
+        if src_rep is not None:
+            tt(u(prod), src_rep, u("R16"), A.mult)
+        mm([(u(ps, 0, 8), u(prod), u(blk))] + [(u(ps, 0, 8), u(a), u(b)) for a, b in extra])
+        cp(u(out), u(ps, 0, 8))
+
+    def part_own(t):
+        cl = t % 4
+        lanes = u("W", 1 + cl, 513, 4)
+        cp(u("OWN"), lanes)
+        cp(u("OWNH"), lanes)
+        ts(u("EO"), lanes, 0.0, A.is_equal)
+        win = u("X", 0, 2064)
+        if t == 0:
+            late = None
+            cp(u("T"), ix(win, u("OWN")))
+        else:
+            cp(u("T"), ix(win, u("OWN")))
+        mm([(u("p4", 0, 128), u("IDB"), u("CK")), (u("p4", 0, 128), u("EO"), u("IDE")), (u("p4", 0, 128), u("OWNH"), u("ID16"))]
+           + sums("p4", 0, "T", "w32k"))
+        scan(u("US"), u("MS", 0, 2048), u("T"), A.mult, A.max)
+        scan(u("S1"), u("MIN"), u("p4", 0, 128), A.max, A.min)
+        ts(u("k8"), u("S1", 15, None, 16), -1.0, A.add)
+        ts(u("sv8"), u("k8"), 2047, A.bitwise_and)
+        ts(u("ZS", 0, None, 16), u("sv8"), 1.0, A.add)
+        hold(u("SR"), u("ZS"))
+        tile(u("SR"), "PS", "blk16", "S16")
+        cp(u("Z", 0, None, 16), ix(win, u("S16")))
+        scan(u("REP"), u("MS", 0, 2048), u("Z"), A.mult, A.add)
+        for c in range(4):
+            a, b = 512 * c, 512 * c + 512
+            mm([(u("p%d" % c), u("IDB"), u("T", a, b)), (u("p%d" % c), u("NIDB"), u("REP", a, b))])
+        mm([(u("p6", 8, 16), u("US", 15, None, 16), u("BD", 0, None, 16))])
+        mm([(u("p5", 128, 256), u("OWNH"), u("ID16x"))])
+        mm([(u("p5", 256, 384), u("OWNH"), u("ID16x")), (u("p5", 256, 384), u("IDB"), u("CKP"))])
+        mm([(u("p7", 0, 8), u("EO"), u("BD", 0, None, 16))])
+        ts(u("sx8"), u("k8"), 15, A.logical_shift_right)
+        ts(u("live8"), u("S1", 15, None, 16), 2.0 ** 23, A.is_lt)
+
+    def part_own_end(t):
+        tt(u("gr8"), u("p6", 8, 16), u("sx8"), A.subtract)
+        tt(u("gr8"), u("gr8"), u("lim28"), A.is_gt)
+        tt(u("wp8"), u("gr8"), u("live8"), A.mult)
+        ts(u("ZN", 0, None, 16), u("p7", 0, 8), -1.0, A.mult, 16.0, A.add)
+
+    def part_own_scalar(t):
+        act(u("SQS"), u("Z", 0, None, 16), F.Square)
+        for c in range(4):
+            act(u("SQ", 512 * c, 512 * c + 512), u("p%d" % c), F.Square)
+        act(u("W16L"), u("p5", 128, 256), F.Copy)
+        act(u("WL"), u("p5", 128, 256), F.Copy, scale=0.0625)
+        act(u("PW2"), u("p5", 256, 384), F.Copy)
+
+    def part_split(t):
+        hold(u("NR"), u("ZN"))
+        tile(u("NR"), "NP", "blk128", "N16", [("ID16", "CI")], ps="p7")
+        mm([(u("p5", 0, 128), u("ID16"), u("KB")), (u("p5", 0, 128), u("EO"), u("NIDE"))] + sums("p5", 0, "SQ", "w2k"))
+        scan(u("SB"), u("MS", 0, 128), u("p5", 0, 128), A.mult, A.max)
+        cp(u("b8"), u("SB", 15, None, 16))
+        ts(u("bb8"), u("b8"), 2047, A.bitwise_and)
+        ts(u("ZBB", 0, None, 16), u("bb8"), -1.0, A.mult, 2047.0, A.add)
+        hold(u("BR"), u("ZBB"))
+        tile(u("BR"), "BP", "blk16", "B16", ps="p7")
+        cp(u("XB"), ix(u("T"), u("B16")))
+        act(u("SQB"), u("XB"), F.Square)
+        tt(u("WV"), u("Z", 0, None, 16), u("XB"), A.subtract)
+        tt(u("AX"), ix(u("WV"), u("CREP")), u("T"), A.mult)
+        mm([(u("p5", 384, 512), u("SQB"), u("BD")), (u("p5", 384, 512), u("SQS"), u("NBD"))] + sums("p5", 384, "AX", "w2"))
+
+    def part_compact(t):
+        ts(u("mb"), u("W16L"), 0.0, A.is_gt)
+        ts(u("lv"), u("p5", 384, 512), 0.0, A.is_lt)
+        tt(u("L1"), u("lv"), u("mb"), A.mult)
+        scan(u("cl"), u("MS", 0, 128), u("L1"), A.mult, A.add)
+        tt(u("SM"), u("mb"), u("L1"), A.subtract)
+        tt(u("q1a"), u("W16L"), u("cl"), A.add)
+        tt(u("q2a"), u("PW2"), u("cl"), A.subtract)
+        tt(u("Pa", 0, 128), u("q1a"), u("SM"), A.mult)
+        tt(u("Pa", 128, 256), u("q2a"), u("L1"), A.mult)
+        a, b = "Pa", "Pb"
+        for s in range(4):
+            ts(u("Mi", 0, 256), u(a, 0, 256), 1 << s, A.bitwise_and)
+            ts(u("p5", 0, 256), u("Mi", 0, 256), 2.0 ** (16 - s), A.mult)
+            tt(u("Aa", 0, 256), u(a, 0, 256), u("p5", 0, 256), A.min)
+            tt(u("p5", 256, 512), u(a, 0, 256), u("p5", 0, 256), A.subtract)
+            tt(u(b, 0, 256), u("p5", 256, 512), u("Aa", 1 << s, 256 + (1 << s)), A.max)
+            a, b = b, a
+        ts(u("STI"), u(a, 0, 256), 4, A.logical_shift_right)
+        tt(u("STM"), u("STI", 0, 128), u("WL"), A.subtract)
+
+    def part_vacant(t):
+        ts(u("VC"), u("W", 1, 513), 0.0, A.is_equal)
+        mm([(u("p7", 0, 32), u("Y", 15 - r, 143 - r), u("VC", r, None, 16)) for r in range(16)])
+        cp(u("VTb"), u("p7", 0, 32))
+        mm([(u("p7", 0, 32), u("BD"), u("VTb"))])
+        mm([(u("p6", 0, 32), u("BT"), u("VTb")), (u("p6", 0, 32), u("ID16"), u("CVn"))])
+        scan(u("CSs"), u("ONEB", 0, 32), u("p7", 0, 32), A.mult, A.add)
+        tt(u("rk"), u("CSs"), u("p6", 0, 32), A.add)
+        tt(u("rk"), u("rk"), u("VTb"), A.mult)
+        tt(u("rk"), u("rk"), u("CVp"), A.add)
+        cp(u("F16"), u("rk"))
+        ts(u("NFH"), u("SEL0"), u("CSs", 31, 32), A.mult)
+        mm([(u("p7", 0, 8), u("ONE16"), u("NFH"))])
+        cp(u("nf8"), u("p7", 0, 8))
+        cp(ix(u("FREE"), u("F16")), u("V0"))
+
+    def part_partner(t):
+        cl = t % 4
+        win = u("X", 0, 2064)
+        i = ix(u("AC4"), u("S16"))
+        ts(u("AN"), i, 1, A.add)
+        act(u("OG"), ix(u("OT", 0, 2064), u("AN")), F.Copy)
+        for h in range(2):
+            a, b = 1024 * h, 1024 * h + 1024
+            tt(u("AX", a, b), ix(win, u("AN", 64 * h, 64 * h + 64)), u("REP", a, b), A.subtract)
+            act(u("SQ", a, b), u("AX", a, b), F.Square)
+        mm([(u("p4", 0, 128), u("ONEB"), u("KA")), (u("p4", 0, 128), u("EO"), u("DEAD"))] + sums("p4", 0, "OG", "og%d" % cl)
+           + sums("p4", 0, "SQ", "w8k"))
+        part_vacant(t)
+        scan(u("S2"), u("MIN"), u("p4", 0, 128), A.max, A.min)
+        cp(u("a8"), u("S2", 15, None, 16))
+        ts(u("has8"), u("S2", 15, None, 16), 14.0e6, A.is_lt)
+        ts(u("d8"), u("a8"), 511, A.bitwise_and)
+        ts(u("dp8"), u("d8"), 1.0, A.add)
+        tt(u("ZD", 0, None, 16), u("dp8"), u("has8"), A.mult)
+        hold(u("D1R"), u("ZD"))
+        tile(u("D1R"), "PD", "blk16", "D16")
+        lists = ix(u("W", 0, 520), u("D16"))
+        cp(u("DM"), lists)
+        act(u("DT", 1024, 2048), ix(win, u("DM", 64, 128)), F.Copy)
+        cp(u("DT", 0, 1024), ix(win, u("DM", 0, 64)))
+        cp(u("DMH"), ix(u("W", 0, 520), u("D16")))
+        ts(u("ED"), u("DM"), 0.0, A.is_equal)
+        ts(u("nD"), u("ZD", 0, None, 16), -1.0, A.mult)
+        tt(u("d18"), u("dp8"), u("has8"), A.mult)
+        for q in range(8):
+            ts(u("DG", 128 * q, 128 * q + 128), u("ID16"), u("d18", q, q + 1), A.mult)
+        for q in range(8):
+            ps = "p%d" % (q // 4)
+            lo = 128 * (q % 4)
+            mm([(u(ps, lo, lo + 128), u("TRI"), u("DG", 128 * q, 128 * q + 128))])
+        mm([(u("p7", 0, 8), u("EO"), u("BD", 0, None, 16)), (u("p7", 0, 8), u("ED"), u("BD", 0, None, 16))])
+        mm([(u("p4", 0, 128), u("ED"), u("ID1K"))] + sums("p4", 0, "DT", "w1"))
+        scan(u("AX"), u("MS", 0, 2048), u("DT"), A.mult, A.max)
+        tt(u("Vv"), u("US", 15, None, 16), u("AX", 15, None, 16), A.max)
+        mm([(u("p6", 0, 8), u("Vv"), u("BD", 0, None, 16))])
+        for q in range(8):
+            ps = "p%d" % (q // 4)
+            lo = 128 * (q % 4)
+            act(u("AB", 128 * q, 128 * q + 128), u(ps, lo, lo + 128), F.Abs, bias=u("nD", q, q + 1))
+        for c in range(4):
+            ps = "p%d" % (2 + c % 2)
+            for k in range(4):
+                s = 4 * c + k
+                mm([(u(ps, 128 * k, 128 * k + 128), u("SH", 128 * s, 128 * s + 128), u("DMH"))])
+            act(u("DS", 512 * c, 512 * c + 512), u(ps), F.Copy)
+        ts(u("sz8"), u("p7", 0, 8), 16.0, A.is_ge)
+        scan(u("S3"), u("MIN"), u("p4", 0, 128), A.max, A.min)
+        tt(u("mn8"), u("S3", 15, None, 16), u("sx8"), A.min)
+        tt(u("tm8"), u("mn8"), u("thr8"), A.add)
+        scan(u("ABS"), u("FM"), u("AB"), A.max, A.min)
+        ts(u("f8"), u("ABS", 127, None, 128), 0.5, A.is_ge)
+        tt(u("P0"), u("f8"), u("has8"), A.mult)
+        tt(u("P0"), u("P0"), u("sz8"), A.mult)
+        cp(u("DSE"), ix(u("DS"), u("N16")))
+
+    def part_finish(t):
+        cl = t % 4
+        zm, zw, zs, zi, zv = [u(z, 0, None, 16) for z in ("ZM", "ZW", "ZSP", "ZI", "ZV")]
+        tt(u("c8"), u("p6", 0, 8), u("tm8"), A.is_le)
+        tt(zm, u("c8"), u("P0"), A.mult)
+        tt(zw, u("wp8"), zm, A.is_gt)
+        hold(u("WR"), u("ZW"))
+        mm([(u("p7", 0, 128), u("TRI"), u("WR"))])
+        hold(u("MR"), u("ZM"))
+        mm([(u("p4", 0, 128), u("MR"), u("ID16"))])
+        tt(u("sp8"), u("p7", 0, 128, 16), u("nf8"), A.is_lt)
+        tt(zs, u("sp8"), zw, A.mult)
+        tt(u("ms8"), zm, zs, A.add)
+        tt(zi, u("live8"), u("ms8"), A.is_gt)
+        hold(u("IR"), u("ZI"))
+        mm([(u("p6", 128, 256), u("TRI"), u("IR"))])
+        hold(u("SPR"), u("ZSP"))
+        tt(u("SPP"), u("SPR"), u("R16"), A.mult)
+        tt(u("KP"), u("p7", 0, 128), u("SPP"), A.mult)
+        ts(u("v8"), u("p6", 128, 256, 16), 32.0, A.is_lt)
+        tt(zv, u("v8"), zi, A.mult)
+        hold(u("VR"), u("ZV"))
+        tt(u("VP"), u("VR"), u("R16"), A.mult)
+        tt(u("NVP"), u("R16"), u("VP"), A.subtract)
+        tt(u("RP"), u("p6", 128, 256), u("VP"), A.mult)
+        tile(None, "RP", "blk16", "RT16", [("NVP", "blk32")])
+        xv = "XV%d" % t
+        cp(ix(u(xv), u("RT16")), u("Z", 0, None, 16))
+        send(T.cores[(rank + 1 + t % 7) % 8], xv, "QI%d" % t, "rq%d" % t, "fq%d" % t, "lq%d" % t, 0)
+        tile(None, "KP", "blk16", "K16", [("SPP", "blkm"), ("IDB", "C640")], ps="p7")
+        cp(u("EV"), ix(u("FREE"), u("K16")))
+        cp(u("EVH"), u("EV"))
+        mm([(u("p7", 0, 128), u("EVH"), u("SEL5"))])
+        tt(u("A2"), u("STM"), u("SPR"), A.mult)
+        tt(u("A3"), u("STI", 128, 256), u("SPR"), A.mult)
+        tt(u("A1"), u("p4", 0, 128), u("DSE"), A.mult)
+        mm([(u("p5", 0, 128), u("ID16"), u("OWNH")), (u("p5", 0, 128), u("ID16"), u("A1")), (u("p5", 0, 128), u("A2"), u("ID16"))])
+        mm([(u("p5", 128, 256), u("A3"), u("ID16"))])
+        tt(u("MD"), u("p4", 0, 128), u("DMH"), A.mult)
+        mm([(u("p3", 0, 128), u("ID16"), u("MD")), (u("p3", 0, 128), u("A3"), u("ID16"))])
+        tt(u("f128a"), u("p4", 0, 128), u("V0", cl, None, 4), A.mult)
+        tt(u("ZE", 0, 2048, 16), u("f128a"), u("EV"), A.add)
+        scan(u("VE", 0, 2048), u("MS", 0, 2048), u("ZE", 0, 2048), A.mult, A.add)
+        ts(u("f128b"), u("p3", 0, 128), 0.0, A.is_equal)
+        tt(u("f128b"), u("f128b"), u("DUM"), A.mult)
+        tt(u("f128b"), u("f128b"), u("p3", 0, 128), A.add)
+        cp(u("MVO"), u("f128b"))
+        act(u("ELS"), u("p5", 128, 256), F.Copy)
+        act(ix(u("OT", 0, 4112), u("MVO")), u("VE", 0, 2048), F.Silu)
+        tt(u("MP"), u("MR"), u("R16"), A.mult)
+        tt(u("Q1"), u("PD"), u("MR"), A.mult)
+        tt(u("Q2"), u("p7", 0, 128), u("SPP"), A.mult)
+        tile(None, "Q1", "blk16", "TG16", [("Q2", "blk16"), ("MP", "blkN"), ("SPP", "blkN"), ("ID16", "C528")])
+        cp(u("W", 1 + cl, 513, 4), u("p5", 0, 128))
+        cp(ix(u("W", 0, 656), u("TG16")), u("ELS"))
+
+    def part_late(t):
+        tt(u("XP"), u("PS"), u("VR"), A.mult)
+        tile(None, "XP", "blk16", "XT16", [("NVP", "blkI"), ("NVP", "blk2k")])
+        if t + 1 < RO:
+            mm([(u("p7", 0, 8), u("ONE16"), u("MR", 0, None, 16))])
+            op("v", lambda: v.tensor_reduce(u("mc", 0, 1)[0], u("p7", 0, 8)[0], AX_.X, A.add), [u("mc", 0, 1)], [u("p7", 0, 8)])
+            cp(u("mci", 0, 1), u("mc", 0, 1))
+            ts(u("mci", 1, 2), u("mci", 0, 1), 15, A.bitwise_and)
+            cp(u("mc", 1, 2), u("mci", 1, 2))
+            ts(u("thr8"), u("lim8"), u("mc", 1, 2), A.add)
+
+    def part_serve(t):
+        src = T.cores[(rank - 1 - t % 7) % 8]
+        n = landed_n(src, 0)
+        qi, sn = "QI%d" % t, "SN%d" % t
+        rq = "rq%d" % t
+        p32 = (0, 32)
+        for e in ("p", "v"):
+            arrived(e, qi, rq, n)
+        mm([(u("p6", 0, 128, 1, p32), u(qi), u("WTB"))])
+        cp(u("QZ", 0, None, 16), u(qi))
+        tt(u("VFP", p=p32), u("p6", 0, 128, 1, p32), u("R16", p=p32), A.mult)
+        mm([(u("p7", 0, 2), u("VFP", p=p32), u("blkf", 0, 2, 1, p32))])
+        cp(u("VI"), u("p7", 0, 2))
+        ts(u("VI2"), u("VI"), 2047, A.bitwise_and)
+        ts(u("VV16"), u("VI2"), 1, A.add)
+        scan(u("QRp"), u("MS", 0, 512), u("QZ"), A.mult, A.add)
+        cp(u("HO"), ix(u("OT", 0, 2064), u("VV16")))
+        mm([(u("p6", 0, 128, 1, p32), u("HO"), u("HWB"))])
+        tt(u("QP", p=p32), u("p6", 0, 128, 1, p32), u("R16", p=p32), A.mult)
+        mm([(u("p7", 0, 2), u("QP", p=p32), u("blk16", 0, 2, 1, p32))])
+        ts(u("H16"), u("p7", 0, 2), -511.0, A.add)
+        cp(u("HL"), ix(u("W", 0, 520), u("H16")))
+        tt(u("QD"), ix(u("X", 0, 2064), u("HL")), u("QRp"), A.subtract)
+        ts(u("EH"), u("HL"), 0.0, A.is_equal)
+        act(u("QS"), u("QD"), F.Square)
+        mm([(u("p6", 0, 128, 1, p32), u("ID16", 0, 32), u("KV")), (u("p6", 0, 128, 1, p32), u("EH"), u("IDE"))]
+           + sums("p6", 0, "QS", "w512", p32))
+        scan(u("QSC", p=p32), u("MIN", p=p32), u("p6", 0, 128, 1, p32), A.max, A.min)
+        cp(u("q8", p=p32), u("QSC", 15, None, 16, p32))
+        ts(u("qq8", p=p32), u("q8", p=p32), 511, A.bitwise_and)
+        cp(u("ZQ", 0, None, 16, p32), u("qq8", p=p32))
+        scan(u("QR8", p=p32), u("MS", 0, 128, 1, p32), u("ZQ", p=p32), A.mult, A.add)
+        tt(u("QP", p=p32), u("QR8", p=p32), u("R16", p=p32), A.mult)
+        mm([(u("p7", 0, 2), u("QP", p=p32), u("blk16", 0, 2, 1, p32))])
+        cp(u("J16"), u("p7", 0, 2))
+        ts(u("hs"), ix(u("QD"), u("J16")), -0.5, A.add, 0.5, A.mult)
+        tt(u(sn), u("hs"), u(qi), A.add)
+        send(src, sn, "RS%d" % t, "rs%d" % t, "fs%d" % t, "ls%d" % t, 1)
+
+    def part_apply(t):
+        src = T.cores[(rank + 1 + t % 7) % 8]
+        arrived("v", "RS%d" % t, "rs%d" % t, landed_n(src, 1))
+        cp(u("RESW", 0, 32), u("RS%d" % t))
+        cp(u("NV"), ix(u("RESW"), u("RT16")))
+        cp(ix(u("X"), u("XT16")), u("NV"))
+
+    part_own(0)
+    late_constants()
+    part_own_end(0)
+    scan(u("VB"), u("MS", 0, NB), u("ZB"), A.mult, A.add)
+    cp(ix(u("OB"), u("INO", CA, 512)), u("VB"))
+    part_own_scalar(0)
+    part_split(0)
+    tt(u("OT", 0, 2064), u("OT", 0, 2064), u("OB", 0, 2064), A.add)
+    part_compact(0)
+    for t in range(RO):
+        part_partner(t)
+        part_finish(t)
+        part_late(t)
+        if t + 1 < RO:
+            part_own(t + 1)
+            part_own_end(t + 1)
+            part_own_scalar(t + 1)
+            part_serve(t)
+            part_split(t + 1)
+            part_compact(t + 1)
+            part_apply(t)
+        else:
+            ts(u("t512a"), u("W", 1, 513), 0.0, A.is_equal, 2049.0, A.mult)
+            ts(u("t512b"), u("W", 1, 513), -1.0, A.add)
+            tt(u("YM"), u("t512a"), u("t512b"), A.add)
+            dma("y", ext(T.ym[:], "out_m"), u("YM"), "st0")
+            part_serve(t)
+            part_apply(t)
+            dma("y", ext(T.yx[:], "out_x"), u("X", 1, 2049), "st1")
+    for sem in total:
+        n = total[sem]
+        if known["k"].get(sem, 0) < n:
+            g.wait_ge(T.sem[sem], n)

@@ -1,8 +1,6 @@
 from concourse.mybir import dt, AluOpType as A, AxisListType as AX_, ActivationFunctionType as F
 
-RO, CA = 5, 256
-CB = 512 - CA
-NA, NB = 16 * CA, 16 * CB
+RO = 5
 BIG = 1.0e9
 S, B, H, I, U = "float32", "bfloat16", "float16", "int32", "uint16"
 
@@ -20,15 +18,14 @@ _sb("MI", 512, I)
 _sb("LI", 2, I)
 _sb("WI", 1, I)
 _sb("W", 664, S)
-_sb("OT", 2064 + NA, S)
-_sb("OB", 2064 + NB, B)
-_sb("VE", max(NA, 2048), S)
-_sb("ZE", max(NA, 2048), B)
-_sb("VB", NB, B)
-_sb("ZB", NB, B)
+_sb("OT", 4112, S)
+_sb("VE VG", 2048, S)
+_sb("VF", 128, S)
+_sb("ZE MS", 2048, B)
 _sb("V0 Jf J2f t512a t512b t512c", 512, S)
 _sb("J3", 512, I)
-_sb("MS", max(NA, 2048), B)
+_sb("Jh", 144, H)
+_sb("J4h J15h", 128, H)
 _sb("MIN", 128, B)
 _sb("FM", 1024, B)
 _sb("T US Z REP SQ AX OG DT", 2048, B)
@@ -51,7 +48,7 @@ _sb("PIi", 4, I)
 _sb("PC", 32, S)
 _sb("J", 512, I)
 _sb("J4 J15", 128, I)
-_sb("blk16 blk128 blkN blkI blk32 blkm blk2k CI C528", 8, H)
+_sb("blk16 blk128 blkN blkE blkI blk32 blkm blk2k CI C528", 8, H)
 _sb("blkf", 8, S)
 _sb("C640 w32k w8k w2k w512 w1 w2 og0 og1 og2 og3 SEL0", 8, B)
 _sb("k8 sv8 sx8 b8 bb8 a8 d8 q8 qq8", 8, I)
@@ -85,7 +82,7 @@ def _pack():
     keep, pos = {}, {}
     big = ("X", "T", "W", "XV", "QI", "SN", "RS")
     for n, (w, sh, d) in SCRATCH.items():
-        if n in ("X", "T", "W", "AC4", "OT", "OB", "FREE", "RESW", "DS", "QD", "WV") or n[:2] in ("XV", "QI", "SN", "RS"):
+        if n in ("X", "T", "W", "AC4", "OT", "VF", "FREE", "RESW", "DS", "QD", "WV") or n[:2] in ("XV", "QI", "SN", "RS"):
             keep[n] = (w, sh, d)
             _ARENA[n] = (n, 0, sh[1], d)
         else:
@@ -312,16 +309,16 @@ def rank_program(g, core, T, topo):
     op("k", lambda: g.iota(u("J3")[0], [[0, 128], [1, 4]], 0, 0), [u("J3")], [])
     op("k", lambda: g.iota(u("Jf")[0], [[1, 512]], 1, 0, allow_small_or_imprecise_dtypes=True), [u("Jf")], [])
     op("k", lambda: g.iota(u("OT", 0, 2064)[0], [[0, 2064]], 0, 0, allow_small_or_imprecise_dtypes=True), [u("OT", 0, 2064)], [])
-    op("k", lambda: g.iota(u("OB", 0, 2064)[0], [[0, 2064]], 0, 0, allow_small_or_imprecise_dtypes=True), [u("OB", 0, 2064)], [])
+    op("k", lambda: g.iota(u("Z")[0], [[0, 2048]], 0, 0, allow_small_or_imprecise_dtypes=True), [u("Z")], [])
 
     fill(u("MS"), 1.0)
     fill(u("MS", 0, None, 16), 0.0)
     fill(u("ZE"), 0.0)
-    fill(u("ZB"), 0.0)
     fill(u("MIN"), -BIG)
     fill(u("MIN", 0, None, 16), BIG)
-    fill(u("W"), 0.0)
-    J, J4, J15 = u("J", 0, 128), u("J4"), u("J15")
+    fill(u("W", 0, 8), 0.0)
+    fill(u("W", 512, 664), 0.0)
+    J, J4, J15 = u("Jh", 0, 128), u("J4h"), u("J15h")
 
     def col(n):
         return u("PC", n, n + 1)
@@ -329,32 +326,38 @@ def rank_program(g, core, T, topo):
     ts(u("PIi", 1, 2), u("PIi", 0, 1), 4, A.logical_shift_right)
     ts(u("PIi", 2, 3), u("PIi", 0, 1), 15, A.bitwise_and)
     cp(u("PC", 0, 3), u("PIi", 0, 3))
-    ts(J4, J, 4, A.logical_shift_right)
-    ts(J15, J, 15, A.bitwise_and)
+    ts(u("J4"), u("J", 0, 128), 4, A.logical_shift_right)
+    ts(u("J15"), u("J", 0, 128), 15, A.bitwise_and)
+    cp(u("Jh"), u("J", 0, 144))
+    cp(J4, u("J4"))
+    cp(J15, u("J15"))
     ts(col(3), P15, 4, A.is_equal)
     ts(col(4), P15, 4, A.is_equal, 128.0, A.mult)
     ts(col(5), P15, 5, A.is_equal)
-    act(u("t512a"), u("J2f"), F.Identity, scale=col(3), bias=col(4))
-    act(u("t512b"), u("Jf"), F.Copy, scale=col(5))
+    ts(col(27), P15, 5, A.is_equal, 1024.0, A.mult)
+    act(u("p4"), u("J2f"), F.Identity, scale=col(3), bias=col(4))
+    act(u("p5"), u("Jf"), F.Identity, scale=col(5), bias=col(27))
     ts(u("t512c"), u("J3"), P15, A.is_equal, 64.0, A.mult)
-    tt(u("t512a"), u("t512a"), u("t512b"), A.add)
-    tt(u("V0"), u("t512a"), u("t512c"), A.add)
-    cp(u("ZE", 0, NA, 16), u("V0", 0, CA))
-    cp(u("ZB", 0, NB, 16), u("V0", CA, 512))
-    scan(u("VE", 0, NA), u("MS", 0, NA), u("ZE", 0, NA), A.mult, A.add)
-    ts(u("t512b"), u("MI"), 2048, A.is_lt)
-    ts(u("t512c"), u("MI"), 1, A.add)
-    tt(u("W", 1, 513), u("t512b"), u("t512c"), A.mult)
+    tt(u("t512c"), u("t512c"), u("p4"), A.add)
+    tt(u("V0"), u("t512c"), u("p5"), A.add)
     ts(col(6), P15, 2064, A.add)
     ts(u("DUM"), J, 16, A.mult, col(6), A.add)
-    ts(u("t512a", 0, CA), u("J", 0, CA), 16, A.mult, col(6), A.add)
-    ts(u("t512a", CA, 512), u("J", 0, CB), 16, A.mult, col(6), A.add)
-    ts(u("t512b"), u("MI"), 2048, A.is_equal)
-    tt(u("t512b"), u("t512b"), u("t512a"), A.mult)
-    tt(u("t512b"), u("t512b"), u("W", 1, 513), A.add)
-    cp(u("INO"), u("t512b"))
-    act(ix(u("OT"), u("INO", 0, CA)), u("VE", 0, NA), F.Silu)
 
+    def owners(c):
+        a, b = 128 * c, 128 * c + 128
+        ve = "VE" if c % 2 == 0 else "VG"
+        cp(u("ZE", 0, None, 16), u("V0", a, b))
+        scan(u(ve), u("MS"), u("ZE"), A.mult, A.add)
+        ts(u("p5", 0, 128), u("MI", a, b), 2048, A.is_equal)
+        tt(u("p5", 128, 256), u("DUM"), u("p5", 0, 128), A.mult)
+        tt(u("f128a"), u("W", 1 + a, 1 + b), u("p5", 128, 256), A.add)
+        cp(u("INO", a, b), u("f128a"))
+        act(ix(u("OT"), u("INO", a, b)), u(ve), F.Silu)
+
+    ts(u("p6"), u("MI"), 2048, A.is_lt)
+    ts(u("t512c"), u("MI"), 1, A.add)
+    tt(u("W", 1, 513), u("t512c"), u("p6"), A.mult)
+    owners(0)
     ts(u("IDB"), J, P, A.is_equal)
     ts(u("NIDB"), J, P, A.is_equal, -1.0, A.mult)
     ts(u("ID16"), J, P, A.is_equal)
@@ -366,6 +369,7 @@ def rank_program(g, core, T, topo):
     ts(u("BD"), J4, P4, A.is_equal)
     ts(u("NBD"), J4, P4, A.is_equal, -1.0, A.mult)
     ts(u("R16"), J15, P15, A.is_equal)
+    ts(u("p3", 0, 128), J15, P15, A.is_equal)
     ts(u("CK"), J15, 2048.0, A.mult)
     ts(u("CKP"), J15, 1.0, A.add)
     ts(u("blk16"), u("J", 0, 8), P4, A.is_equal)
@@ -376,7 +380,7 @@ def rank_program(g, core, T, topo):
     ts(u("w512"), u("BD", 0, None, 16), 512.0, A.mult)
     ts(u("w1"), u("BD", 0, None, 16), 1.0, A.mult)
     ts(u("w2"), u("BD", 0, None, 16), 2.0, A.mult)
-    fill(u("Z"), 0.0)
+    owners(1)
     for z in "ZS ZD ZN ZBB ZM ZW ZSP ZI ZV ZQ".split():
         ts(u(z), J, 0.0, A.mult)
 
@@ -408,6 +412,8 @@ def rank_program(g, core, T, topo):
         ts(u("blk128"), u("J", 0, 8), P4, A.is_equal, 128.0, A.mult)
         ts(col(16), P, -1.0, A.mult, -528.0, A.add)
         ts(u("blkN"), u("J", 0, 8), P4, A.is_equal, col(16), A.mult)
+        ts(col(28), P, -1.0, A.mult, -1552.0, A.add)
+        ts(u("blkE"), u("J", 0, 8), P4, A.is_equal, col(28), A.mult)
         ts(col(17), P, 16.0, A.add)
         ts(u("blkI"), u("J", 0, 8), P4, A.is_equal, col(17), A.mult)
         ts(col(18), P, 32.0, A.add)
@@ -429,6 +435,7 @@ def rank_program(g, core, T, topo):
         ts(u("CVp"), u("J", 0, 32), 16.0, A.mult, col(22), A.add)
         ts(u("CVn"), u("CVp"), -1.0, A.mult)
         fill(u("FREE"), 0.0)
+        fill(u("STI", 0, 8), 0)
         fill(u("DS", 2048, 2176), 0.0)
         fill(u("RESW"), 0)
         fill(u("QZ"), 0.0)
@@ -451,7 +458,7 @@ def rank_program(g, core, T, topo):
 
     def tile(src_rep, prod, blk, out, extra=(), ps="p6"):
         if src_rep is not None:
-            tt(u(prod), src_rep, u("R16"), A.mult)
+            tt(u(prod), src_rep, u("p3", 0, 128), A.mult)
         mm([(u(ps, 0, 8), u(prod), u(blk))] + [(u(ps, 0, 8), u(a), u(b)) for a, b in extra])
         cp(u(out), u(ps, 0, 8))
 
@@ -459,52 +466,63 @@ def rank_program(g, core, T, topo):
         cl = t % 4
         lanes = u("W", 1 + cl, 513, 4)
         cp(u("OWN"), lanes)
-        cp(u("OWNH"), lanes)
-        ts(u("EO"), lanes, 0.0, A.is_equal)
         win = u("X", 0, 2064)
         if t == 0:
-            late = None
             cp(u("T"), ix(win, u("OWN")))
         else:
-            cp(u("T"), ix(win, u("OWN")))
+            act(u("T", 1024, 2048), ix(win, u("OWN", 64, 128)), F.Copy)
+            cp(u("T", 0, 1024), ix(win, u("OWN", 0, 64)))
+        ts(u("EO"), lanes, 0.0, A.is_equal)
+        cp(u("OWNH"), lanes)
+        ts(u("VC"), u("W", 1, 513), 0.0, A.is_equal)
         mm([(u("p4", 0, 128), u("IDB"), u("CK")), (u("p4", 0, 128), u("EO"), u("IDE")), (u("p4", 0, 128), u("OWNH"), u("ID16"))]
            + sums("p4", 0, "T", "w32k"))
         scan(u("US"), u("MS", 0, 2048), u("T"), A.mult, A.max)
+        mm([(u("p7", 32, 40), u("EO"), u("BD", 0, None, 16))])
+        mm([(u("p5", 128, 256), u("OWNH"), u("ID16x"))])
+        mm([(u("p5", 256, 384), u("OWNH"), u("ID16x")), (u("p5", 256, 384), u("IDB"), u("CKP"))])
+        mm([(u("p6", 8, 16), u("US", 15, None, 16), u("BD", 0, None, 16))])
         scan(u("S1"), u("MIN"), u("p4", 0, 128), A.max, A.min)
         ts(u("k8"), u("S1", 15, None, 16), -1.0, A.add)
         ts(u("sv8"), u("k8"), 2047, A.bitwise_and)
+        ts(u("sx8"), u("k8"), 15, A.logical_shift_right)
         ts(u("ZS", 0, None, 16), u("sv8"), 1.0, A.add)
+        ts(u("live8"), u("S1", 15, None, 16), 2.0 ** 23, A.is_lt)
         hold(u("SR"), u("ZS"))
         tile(u("SR"), "PS", "blk16", "S16")
         cp(u("Z", 0, None, 16), ix(win, u("S16")))
-        scan(u("REP"), u("MS", 0, 2048), u("Z"), A.mult, A.add)
-        for c in range(4):
-            a, b = 512 * c, 512 * c + 512
-            mm([(u("p%d" % c), u("IDB"), u("T", a, b)), (u("p%d" % c), u("NIDB"), u("REP", a, b))])
-        mm([(u("p6", 8, 16), u("US", 15, None, 16), u("BD", 0, None, 16))])
-        mm([(u("p5", 128, 256), u("OWNH"), u("ID16x"))])
-        mm([(u("p5", 256, 384), u("OWNH"), u("ID16x")), (u("p5", 256, 384), u("IDB"), u("CKP"))])
-        mm([(u("p7", 0, 8), u("EO"), u("BD", 0, None, 16))])
-        ts(u("sx8"), u("k8"), 15, A.logical_shift_right)
-        ts(u("live8"), u("S1", 15, None, 16), 2.0 ** 23, A.is_lt)
-
-    def part_own_end(t):
+        mm([(u("p7", 0, 32), u("Y", 15 - r, 143 - r), u("VC", r, None, 16)) for r in range(16)] if t else
+           [(u("p7", 0, 32), u("IDB"), u("VC", 0, 32))])
+        ts(u("ZN", 0, None, 16), u("p7", 32, 40), -1.0, A.mult, 16.0, A.add)
         tt(u("gr8"), u("p6", 8, 16), u("sx8"), A.subtract)
-        tt(u("gr8"), u("gr8"), u("lim28"), A.is_gt)
-        tt(u("wp8"), u("gr8"), u("live8"), A.mult)
-        ts(u("ZN", 0, None, 16), u("p7", 0, 8), -1.0, A.mult, 16.0, A.add)
+        scan(u("REP"), u("MS", 0, 2048), u("Z"), A.mult, A.add)
 
-    def part_own_scalar(t):
+    def dif(c):
+        a, b = 512 * c, 512 * c + 512
+        ps = "p%d" % (c % 3)
+        mm([(u(ps), u("IDB"), u("T", a, b)), (u(ps), u("NIDB"), u("REP", a, b))])
+        act(u("SQ", a, b), u(ps), F.Square)
+
+    def part_own_squares(t):
+        for c in (2, 3):
+            dif(c)
         act(u("SQS"), u("Z", 0, None, 16), F.Square)
-        for c in range(4):
-            act(u("SQ", 512 * c, 512 * c + 512), u("p%d" % c), F.Square)
         act(u("W16L"), u("p5", 128, 256), F.Copy)
         act(u("WL"), u("p5", 128, 256), F.Copy, scale=0.0625)
         act(u("PW2"), u("p5", 256, 384), F.Copy)
 
-    def part_split(t):
+    def part_own_end(t):
+        tt(u("gr8"), u("gr8"), u("lim28"), A.is_gt)
+        tt(u("wp8"), u("gr8"), u("live8"), A.mult)
+
+    def part_sizes(t):
         hold(u("NR"), u("ZN"))
-        tile(u("NR"), "NP", "blk128", "N16", [("ID16", "CI")], ps="p7")
+        tt(u("NP"), u("NR"), u("p3", 0, 128), A.mult)
+        mm([(u("p4", 264, 272), u("NP"), u("blk128")), (u("p4", 264, 272), u("ID16"), u("CI"))])
+
+    def part_split(t):
+        cp(u("N16"), u("p4", 264, 272))
+        cp(u("nf8"), u("p4", 256, 264))
         mm([(u("p5", 0, 128), u("ID16"), u("KB")), (u("p5", 0, 128), u("EO"), u("NIDE"))] + sums("p5", 0, "SQ", "w2k"))
         scan(u("SB"), u("MS", 0, 128), u("p5", 0, 128), A.mult, A.max)
         cp(u("b8"), u("SB", 15, None, 16))
@@ -520,54 +538,66 @@ def rank_program(g, core, T, topo):
 
     def part_compact(t):
         ts(u("mb"), u("W16L"), 0.0, A.is_gt)
-        ts(u("lv"), u("p5", 384, 512), 0.0, A.is_lt)
-        tt(u("L1"), u("lv"), u("mb"), A.mult)
-        scan(u("cl"), u("MS", 0, 128), u("L1"), A.mult, A.add)
+        ts(u("p5", 0, 128), u("p5", 384, 512), 0.0, A.is_lt)
+        tt(u("L1"), u("mb"), u("p5", 0, 128), A.mult)
+        scan(u("p5", 128, 256), u("MS", 0, 128), u("L1"), A.mult, A.add)
         tt(u("SM"), u("mb"), u("L1"), A.subtract)
-        tt(u("q1a"), u("W16L"), u("cl"), A.add)
-        tt(u("q2a"), u("PW2"), u("cl"), A.subtract)
-        tt(u("Pa", 0, 128), u("q1a"), u("SM"), A.mult)
-        tt(u("Pa", 128, 256), u("q2a"), u("L1"), A.mult)
-        a, b = "Pa", "Pb"
-        for s in range(4):
+        tt(u("p5", 0, 128), u("PW2"), u("p5", 128, 256), A.subtract)
+        tt(u("p5", 256, 384), u("W16L"), u("p5", 128, 256), A.add)
+        tt(u("Pa", 128, 256), u("L1"), u("p5", 0, 128), A.mult)
+        tt(u("Pa", 0, 128), u("SM"), u("p5", 256, 384), A.mult)
+
+    def part_shift(t, steps):
+        for s in steps:
+            a, b = ("Pa", "Pb") if s % 2 == 0 else ("Pb", "Pa")
             ts(u("Mi", 0, 256), u(a, 0, 256), 1 << s, A.bitwise_and)
             ts(u("p5", 0, 256), u("Mi", 0, 256), 2.0 ** (16 - s), A.mult)
-            tt(u("Aa", 0, 256), u(a, 0, 256), u("p5", 0, 256), A.min)
             tt(u("p5", 256, 512), u(a, 0, 256), u("p5", 0, 256), A.subtract)
+            tt(u("Aa", 0, 256), u(a, 0, 256), u("p5", 0, 256), A.min)
             tt(u(b, 0, 256), u("p5", 256, 512), u("Aa", 1 << s, 256 + (1 << s)), A.max)
-            a, b = b, a
-        ts(u("STI"), u(a, 0, 256), 4, A.logical_shift_right)
-        tt(u("STM"), u("STI", 0, 128), u("WL"), A.subtract)
+        if 3 in steps:
+            ts(u("STI"), u("Pa", 0, 256), 4, A.logical_shift_right)
+            tt(u("STM"), u("STI", 0, 128), u("WL"), A.subtract)
 
-    def part_vacant(t):
-        ts(u("VC"), u("W", 1, 513), 0.0, A.is_equal)
-        mm([(u("p7", 0, 32), u("Y", 15 - r, 143 - r), u("VC", r, None, 16)) for r in range(16)])
+    def move_owners():
+        act(ix(u("OT", 0, 4112), u("MVO")), u("VE"), F.Silu)
+
+    def part_vacant_count(t):
+        if t == 0:
+            mm([(u("p7", 0, 32), u("Y", 15 - r, 143 - r), u("VC", r, None, 16)) for r in range(16)])
         cp(u("VTb"), u("p7", 0, 32))
         mm([(u("p7", 0, 32), u("BD"), u("VTb"))])
         mm([(u("p6", 0, 32), u("BT"), u("VTb")), (u("p6", 0, 32), u("ID16"), u("CVn"))])
+        part_sizes(t)
+
+    def part_vacant(t):
         scan(u("CSs"), u("ONEB", 0, 32), u("p7", 0, 32), A.mult, A.add)
         tt(u("rk"), u("CSs"), u("p6", 0, 32), A.add)
         tt(u("rk"), u("rk"), u("VTb"), A.mult)
         tt(u("rk"), u("rk"), u("CVp"), A.add)
         cp(u("F16"), u("rk"))
         ts(u("NFH"), u("SEL0"), u("CSs", 31, 32), A.mult)
-        mm([(u("p7", 0, 8), u("ONE16"), u("NFH"))])
-        cp(u("nf8"), u("p7", 0, 8))
-        cp(ix(u("FREE"), u("F16")), u("V0"))
+        mm([(u("p4", 256, 264), u("ONE16"), u("NFH"))])
 
-    def part_partner(t):
+    def part_near(t):
         cl = t % 4
         win = u("X", 0, 2064)
         i = ix(u("AC4"), u("S16"))
         ts(u("AN"), i, 1, A.add)
         act(u("OG"), ix(u("OT", 0, 2064), u("AN")), F.Copy)
+
+    def part_distances(t):
+        cl = t % 4
+        win = u("X", 0, 2064)
         for h in range(2):
             a, b = 1024 * h, 1024 * h + 1024
             tt(u("AX", a, b), ix(win, u("AN", 64 * h, 64 * h + 64)), u("REP", a, b), A.subtract)
             act(u("SQ", a, b), u("AX", a, b), F.Square)
         mm([(u("p4", 0, 128), u("ONEB"), u("KA")), (u("p4", 0, 128), u("EO"), u("DEAD"))] + sums("p4", 0, "OG", "og%d" % cl)
            + sums("p4", 0, "SQ", "w8k"))
-        part_vacant(t)
+
+    def part_partner(t):
+        win = u("X", 0, 2064)
         scan(u("S2"), u("MIN"), u("p4", 0, 128), A.max, A.min)
         cp(u("a8"), u("S2", 15, None, 16))
         ts(u("has8"), u("S2", 15, None, 16), 14.0e6, A.is_lt)
@@ -600,11 +630,12 @@ def rank_program(g, core, T, topo):
             lo = 128 * (q % 4)
             act(u("AB", 128 * q, 128 * q + 128), u(ps, lo, lo + 128), F.Abs, bias=u("nD", q, q + 1))
         for c in range(4):
-            ps = "p%d" % (2 + c % 2)
+            ps = "p%d" % (2 - 2 * (c % 2))
             for k in range(4):
                 s = 4 * c + k
                 mm([(u(ps, 128 * k, 128 * k + 128), u("SH", 128 * s, 128 * s + 128), u("DMH"))])
             act(u("DS", 512 * c, 512 * c + 512), u(ps), F.Copy)
+        act(ix(u("FREE"), u("F16")), u("V0"), F.Silu)
         ts(u("sz8"), u("p7", 0, 8), 16.0, A.is_ge)
         scan(u("S3"), u("MIN"), u("p4", 0, 128), A.max, A.min)
         tt(u("mn8"), u("S3", 15, None, 16), u("sx8"), A.min)
@@ -613,7 +644,6 @@ def rank_program(g, core, T, topo):
         ts(u("f8"), u("ABS", 127, None, 128), 0.5, A.is_ge)
         tt(u("P0"), u("f8"), u("has8"), A.mult)
         tt(u("P0"), u("P0"), u("sz8"), A.mult)
-        cp(u("DSE"), ix(u("DS"), u("N16")))
 
     def part_finish(t):
         cl = t % 4
@@ -631,15 +661,15 @@ def rank_program(g, core, T, topo):
         tt(zi, u("live8"), u("ms8"), A.is_gt)
         hold(u("IR"), u("ZI"))
         mm([(u("p6", 128, 256), u("TRI"), u("IR"))])
-        hold(u("SPR"), u("ZSP"))
-        tt(u("SPP"), u("SPR"), u("R16"), A.mult)
+        hold(u("p3", 128, 256), u("ZSP"))
+        tt(u("SPP"), u("R16"), u("p3", 128, 256), A.mult)
         tt(u("KP"), u("p7", 0, 128), u("SPP"), A.mult)
         ts(u("v8"), u("p6", 128, 256, 16), 32.0, A.is_lt)
         tt(zv, u("v8"), zi, A.mult)
-        hold(u("VR"), u("ZV"))
-        tt(u("VP"), u("VR"), u("R16"), A.mult)
-        tt(u("NVP"), u("R16"), u("VP"), A.subtract)
+        hold(u("p3", 256, 384), u("ZV"))
+        tt(u("VP"), u("R16"), u("p3", 256, 384), A.mult)
         tt(u("RP"), u("p6", 128, 256), u("VP"), A.mult)
+        tt(u("NVP"), u("p3", 0, 128), u("VP"), A.subtract)
         tile(None, "RP", "blk16", "RT16", [("NVP", "blk32")])
         xv = "XV%d" % t
         cp(ix(u(xv), u("RT16")), u("Z", 0, None, 16))
@@ -648,31 +678,31 @@ def rank_program(g, core, T, topo):
         cp(u("EV"), ix(u("FREE"), u("K16")))
         cp(u("EVH"), u("EV"))
         mm([(u("p7", 0, 128), u("EVH"), u("SEL5"))])
-        tt(u("A2"), u("STM"), u("SPR"), A.mult)
-        tt(u("A3"), u("STI", 128, 256), u("SPR"), A.mult)
-        tt(u("A1"), u("p4", 0, 128), u("DSE"), A.mult)
-        mm([(u("p5", 0, 128), u("ID16"), u("OWNH")), (u("p5", 0, 128), u("ID16"), u("A1")), (u("p5", 0, 128), u("A2"), u("ID16"))])
+        tt(u("f128a"), u("p4", 0, 128), u("V0", cl, None, 4), A.mult)
+        tt(u("VF"), u("f128a"), u("EV"), A.add)
+        act(u("VE"), ix(u("VF"), u("CREP")), F.Copy)
+        tt(u("A3"), u("STI", 128, 256), u("p3", 128, 256), A.mult)
         mm([(u("p5", 128, 256), u("A3"), u("ID16"))])
         tt(u("MD"), u("p4", 0, 128), u("DMH"), A.mult)
-        mm([(u("p3", 0, 128), u("ID16"), u("MD")), (u("p3", 0, 128), u("A3"), u("ID16"))])
-        tt(u("f128a"), u("p4", 0, 128), u("V0", cl, None, 4), A.mult)
-        tt(u("ZE", 0, 2048, 16), u("f128a"), u("EV"), A.add)
-        scan(u("VE", 0, 2048), u("MS", 0, 2048), u("ZE", 0, 2048), A.mult, A.add)
-        ts(u("f128b"), u("p3", 0, 128), 0.0, A.is_equal)
-        tt(u("f128b"), u("f128b"), u("DUM"), A.mult)
-        tt(u("f128b"), u("f128b"), u("p3", 0, 128), A.add)
+        mm([(u("p2", 0, 128), u("ID16"), u("MD")), (u("p2", 0, 128), u("A3"), u("ID16"))])
+        cp(u("DSE"), ix(u("DS"), u("N16")))
+        tt(u("A1"), u("p4", 0, 128), u("DSE"), A.mult)
+        tt(u("A2"), u("STM"), u("p3", 128, 256), A.mult)
+        mm([(u("p5", 0, 128), u("ID16"), u("OWNH")), (u("p5", 0, 128), u("ID16"), u("A1")), (u("p5", 0, 128), u("A2"), u("ID16"))])
+        ts(u("p3", 384, 512), u("p2", 0, 128), 0.0, A.is_equal)
+        tt(u("f128b"), u("DUM"), u("p3", 384, 512), A.mult)
+        tt(u("f128b"), u("f128b"), u("p2", 0, 128), A.add)
         cp(u("MVO"), u("f128b"))
-        act(u("ELS"), u("p5", 128, 256), F.Copy)
-        act(ix(u("OT", 0, 4112), u("MVO")), u("VE", 0, 2048), F.Silu)
-        tt(u("MP"), u("MR"), u("R16"), A.mult)
+        tt(u("MP"), u("MR"), u("p3", 0, 128), A.mult)
         tt(u("Q1"), u("PD"), u("MR"), A.mult)
         tt(u("Q2"), u("p7", 0, 128), u("SPP"), A.mult)
-        tile(None, "Q1", "blk16", "TG16", [("Q2", "blk16"), ("MP", "blkN"), ("SPP", "blkN"), ("ID16", "C528")])
+        cp(u("ELS"), u("p5", 128, 256))
+        tile(None, "Q1", "blk16", "TG16", [("Q2", "blk16"), ("MP", "blkN"), ("SPP", "blkE"), ("ID16", "C528")])
         cp(u("W", 1 + cl, 513, 4), u("p5", 0, 128))
         cp(ix(u("W", 0, 656), u("TG16")), u("ELS"))
 
     def part_late(t):
-        tt(u("XP"), u("PS"), u("VR"), A.mult)
+        tt(u("XP"), u("PS"), u("p3", 256, 384), A.mult)
         tile(None, "XP", "blk16", "XT16", [("NVP", "blkI"), ("NVP", "blk2k")])
         if t + 1 < RO:
             mm([(u("p7", 0, 8), u("ONE16"), u("MR", 0, None, 16))])
@@ -707,6 +737,11 @@ def rank_program(g, core, T, topo):
         tt(u("QD"), ix(u("X", 0, 2064), u("HL")), u("QRp"), A.subtract)
         ts(u("EH"), u("HL"), 0.0, A.is_equal)
         act(u("QS"), u("QD"), F.Square)
+
+    def part_serve_met(t):
+        src = T.cores[(rank - 1 - t % 7) % 8]
+        qi, sn = "QI%d" % t, "SN%d" % t
+        p32 = (0, 32)
         mm([(u("p6", 0, 128, 1, p32), u("ID16", 0, 32), u("KV")), (u("p6", 0, 128, 1, p32), u("EH"), u("IDE"))]
            + sums("p6", 0, "QS", "w512", p32))
         scan(u("QSC", p=p32), u("MIN", p=p32), u("p6", 0, 128, 1, p32), A.max, A.min)
@@ -729,32 +764,47 @@ def rank_program(g, core, T, topo):
         cp(ix(u("X"), u("XT16")), u("NV"))
 
     part_own(0)
+    dif(0)
+    dif(1)
+    part_own_squares(0)
+    owners(2)
     late_constants()
     part_own_end(0)
-    scan(u("VB"), u("MS", 0, NB), u("ZB"), A.mult, A.add)
-    cp(ix(u("OB"), u("INO", CA, 512)), u("VB"))
-    part_own_scalar(0)
+    owners(3)
+    part_vacant_count(0)
+    part_vacant(0)
     part_split(0)
-    tt(u("OT", 0, 2064), u("OT", 0, 2064), u("OB", 0, 2064), A.add)
-    part_compact(0)
     for t in range(RO):
+        part_near(t)
+        part_compact(t)
+        part_shift(t, (0, 1))
+        if t:
+            part_apply(t - 1)
+        part_distances(t)
+        part_shift(t, (2, 3))
         part_partner(t)
         part_finish(t)
         part_late(t)
         if t + 1 < RO:
             part_own(t + 1)
+            move_owners()
+            part_vacant_count(t + 1)
+            dif(0)
+            dif(1)
             part_own_end(t + 1)
-            part_own_scalar(t + 1)
+            part_vacant(t + 1)
             part_serve(t)
+            part_own_squares(t + 1)
+            part_serve_met(t)
             part_split(t + 1)
-            part_compact(t + 1)
-            part_apply(t)
         else:
+            move_owners()
             ts(u("t512a"), u("W", 1, 513), 0.0, A.is_equal, 2049.0, A.mult)
             ts(u("t512b"), u("W", 1, 513), -1.0, A.add)
             tt(u("YM"), u("t512a"), u("t512b"), A.add)
             dma("y", ext(T.ym[:], "out_m"), u("YM"), "st0")
             part_serve(t)
+            part_serve_met(t)
             part_apply(t)
             dma("y", ext(T.yx[:], "out_x"), u("X", 1, 2049), "st1")
     for sem in total:

from concourse.mybir import dt, AluOpType as A, AxisListType as AX_, ActivationFunctionType as F

RO = 5
BIG = 1.0e9
S, B, H, I, U = "float32", "bfloat16", "float16", "int32", "uint16"

SCRATCH = {}


def _sb(names, cols, dtype):
    for n in names.split():
        SCRATCH[n] = ("sbuf", [128, cols], dtype)


_sb("X", 2304, B)
_sb("AC4", 2064, I)
_sb("MI", 512, I)
_sb("LI", 2, I)
_sb("WI", 1, I)
_sb("W", 664, S)
_sb("OT", 4112, S)
_sb("VE VG", 2048, S)
_sb("VF", 128, S)
_sb("ZE MS", 2048, B)
_sb("V0 Jf J2f t512a t512b t512c", 512, S)
_sb("J3", 512, I)
_sb("Jh", 144, H)
_sb("J4h J15h", 128, H)
_sb("MIN", 128, B)
_sb("FM", 1024, B)
_sb("T US Z REP SQ AX OG DT", 2048, B)
_sb("DS", 2176, S)
_sb("OWN AN DM CREP MVO", 128, U)
_sb("INO", 512, U)
_sb("OWNH DMH DSE R16 ID16 ID16x NID16 TRI D1R PD KB KV SEL5 SR PS MR MP WR SPR SPP IR VR VP NVP KP RP EVH Q1 Q2 "
    "A1 A2 A3 MD NR NP BR BP XP", 128, H)
_sb("ZS ZD ZN ZBB ZM ZW ZSP ZI ZV ZQ QR8 QP", 128, H)
_sb("EO ED IDB NIDB BD NBD BT IDE NIDE ID1K CK CKP KA DEAD HWB WTB ONEB Vv WV XB SQS SQB NV", 128, B)
_sb("ONE16", 128, H)
_sb("Y", 144, B)
_sb("S1 S2 S3 SB W16L WL PW2 lv mb L1 cl SM q1a q2a STM EV ELS DUM f128a f128b VFP QPF QSC", 128, S)
_sb("Pa Pb Mi Aa", 264, I)
_sb("STI", 256, I)
_sb("DG", 1024, H)
_sb("AB ABS", 1024, B)
_sb("SH", 2048, B)
_sb("PIi", 4, I)
_sb("PC", 32, S)
_sb("J", 512, I)
_sb("J4 J15", 128, I)
_sb("blk16 blk128 blkN blkE blkI blk32 blkm blk2k CI C528", 8, H)
_sb("blkf", 8, S)
_sb("C640 w32k w8k w2k w512 w1 w2 og0 og1 og2 og3 SEL0", 8, B)
_sb("k8 sv8 sx8 b8 bb8 a8 d8 q8 qq8", 8, I)
_sb("lim8 lim28 thr8 live8 gr8 wp8 has8 dp8 nD d18 mn8 tm8 f8 sz8 P0 c8 sp8 ms8 v8 nf8 nfs8", 8, S)
_sb("S16 B16 D16 N16 K16 TG16 RT16 XT16", 8, U)
_sb("NFH", 8, H)
_sb("VC", 512, B)
_sb("VTb", 32, B)
_sb("CSs CVp rk", 32, S)
_sb("CVn", 32, H)
_sb("F16", 32, U)
_sb("FREE", 1168, S)
_sb("mc", 4, S)
_sb("mci", 4, I)
_sb("RESW", 160, I)
_sb("HO EH", 32, B)
_sb("HL", 32, U)
_sb("VI VI2", 2, I)
_sb("VV16 H16 J16", 2, U)
_sb("QZ QRp QD QS", 512, B)
_sb("hs", 32, S)
_sb("YM", 512, S)
for _t in range(RO):
    _sb("XV%d" % _t, 160, B)
    _sb("QI%d" % _t, 32, B)
    _sb("SN%d RS%d" % (_t, _t), 32, I)
_ARENA = {}


def _pack():
    keep, pos = {}, {}
    big = ("X", "T", "W", "XV", "QI", "SN", "RS")
    for n, (w, sh, d) in SCRATCH.items():
        if n in ("X", "T", "W", "AC4", "OT", "VF", "FREE", "RESW", "DS", "QD", "WV") or n[:2] in ("XV", "QI", "SN", "RS"):
            keep[n] = (w, sh, d)
            _ARENA[n] = (n, 0, sh[1], d)
        else:
            c = -(-sh[1] // 16) * 16
            o = pos.get(d, 0)
            _ARENA[n] = ("ar_" + d, o, sh[1], d)
            pos[d] = o + c
    for d in pos:
        keep["ar_" + d] = ("sbuf", [128, pos[d]], d)
    return keep


SCRATCH = _pack()
for _k in range(8):
    SCRATCH["p%d" % _k] = ("psum", [128, 512], S)
    _ARENA["p%d" % _k] = ("p%d" % _k, 0, 512, S)
SEMAPHORES = ["v", "p", "s", "k"] + ["ld%d" % i for i in range(8)] + ["st0", "st1"]
for _t in range(RO):
    SEMAPHORES += ["rq%d" % _t, "rs%d" % _t, "lq%d" % _t, "ls%d" % _t, "fq%d" % _t, "fs%d" % _t, "mq%d" % _t, "ms%d" % _t]


def _mask(topo, a, b):
    es = topo.engines(a, b)[:8]
    return sum(1 << e for e in es), len(es)


def _relay(topo, a, b, which):
    if topo.may_write(a, b):
        return None
    c = [h for h in topo.cores_of(a) if h != a and topo.may_write(h, b)]
    c.sort(key=lambda h: (topo.die(h) != topo.die(a), h))
    return c[which % len(c)]


def _relay_program(g, core, T, topo):
    used = []
    for t in range(RO):
        for r in range(8):
            a, b = T.cores[r], T.cores[(r + 1 + t % 7) % 8]
            for (x, y, buf, arr, fwd, loc, which) in ((a, b, "QI", "rq", "fq", "mq", 0), (b, a, "RS", "rs", "fs", "ms", 1)):
                if _relay(topo, x, y, which) == core:
                    _, n = _mask(topo, x, core)
                    m, n2 = _mask(topo, core, y)
                    rid, pid = topo.addr(y, core)
                    g.wait_ge(T.sem["%s%d" % (fwd, t)], n)
                    g.remote_dma(T["%s%d" % (buf, t)][:], T["%s%d" % (buf, t)][:], T.sem["%s%d" % (arr, t)],
                                 T.sem["%s%d" % (loc, t)], pid, rid, m)
                    used.append((T.sem["%s%d" % (loc, t)], n2))
    for s, n in used:
        g.wait_ge(s, n)


def rank_program(g, core, T, topo):
    rank = T.rank_of(core)
    if rank is None:
        _relay_program(g, core, T, topo)
        return
    E = {"v": g.vector, "p": g.tensor, "s": g.scalar, "k": g, "y": g.sync}
    cnt = {"v": 0, "p": 0, "s": 0, "k": 0}
    known = {e: {} for e in E}
    snap = {}
    log = {}
    total = {}

    def u(name, lo=0, hi=None, st=1, p=None):
        buf, o, n, _d = _ARENA[name]
        hi = n if hi is None else hi
        a, b = o + lo, o + hi
        rows = slice(None) if p is None else slice(p[0], p[1])
        t = T[buf]
        ap = t[rows, a:b:st] if st != 1 else t[rows, a:b]
        return (ap, [(buf, a, b)])

    def ix(win, off):
        return (win[0].indirect(off[0]), win[1] + off[1])

    def need(e, reads, writes):
        w = {}

        def add(sem, val):
            if w.get(sem, 0) < val:
                w[sem] = val
        for kind, lst in ((0, reads), (1, writes)):
            for (b, lo, hi) in lst:
                psum = len(b) == 2 and b[0] == "p"
                for (l2, h2, e2, sem, val, wr) in log.get(b, ()):
                    if psum:
                        if e2 == e:
                            if not (wr and e != "p") or (kind == 1 and not wr) or not (lo < h2 and l2 < hi):
                                continue
                        add(sem, val)
                    elif lo < h2 and l2 < hi and (kind or wr):
                        if e2 == e and e in ("v", "s", "p") and not wr:
                            continue
                        add(sem, val)
        return w

    def wait(e, w):
        for sem in w:
            if known[e].get(sem, 0) < w[sem]:
                E[e].wait_ge(T.sem[sem], w[sem])
                known[e][sem] = w[sem]
                for s2, v2 in snap.get((sem, w[sem]), {}).items():
                    if known[e].get(s2, 0) < v2:
                        known[e][s2] = v2

    def note(e, reads, writes, sem, val):
        d = dict(known[e])
        d[sem] = max(d.get(sem, 0), val)
        snap[(sem, val)] = d
        total[sem] = val
        for (b, lo, hi) in writes:
            old = log.get(b, [])
            log[b] = [x for x in old if not (lo <= x[0] and x[1] <= hi)] + [(lo, hi, e, sem, val, True)]
        for (b, lo, hi) in reads:
            old = log.get(b, [])
            log[b] = [x for x in old if not (x[2] == e and not x[5] and lo <= x[0] and x[1] <= hi and x[3] == sem)] + [(lo, hi, e, sem, val, False)]

    def op(e, fn, outs, ins, dma=None):
        rd = [r for x in ins for r in x[1]]
        wr = [r for x in outs for r in x[1]]
        wait(e, need(e, rd, wr))
        i = fn()
        if dma:
            i.then_inc(T.sem[dma], 16)
            note(e, rd, wr, dma, 16)
        else:
            cnt[e] += 1
            i.then_inc(T.sem[e], 1)
            note(e, rd, wr, e, cnt[e])

    def _c(x):
        return x[0] if isinstance(x, tuple) else x

    def _r(*xs):
        return [x for x in xs if isinstance(x, tuple)]

    v, sc = g.vector, g.scalar

    def cp(o, i, scatter=None):
        op("v", lambda: v.tensor_copy(o[0], i[0]), [o], [i] + (scatter or []))

    def ts(o, i, s1, o1, s2=None, o2=None):
        if o2 is None:
            op("v", lambda: v.tensor_scalar(o[0], i[0], _c(s1), None, o1), [o], [i] + _r(s1))
        else:
            op("v", lambda: v.tensor_scalar(o[0], i[0], _c(s1), _c(s2), o1, o2), [o], [i] + _r(s1, s2))

    def tt(o, a, b, o1):
        op("v", lambda: v.tensor_tensor(o[0], a[0], b[0], o1), [o], [a, b])

    def scan(o, a, b, o1, o2):
        op("v", lambda: v.tensor_tensor_scan(o[0], a[0], b[0], 0.0, o1, o2), [o], [a, b])

    def fill(o, c):
        op("v", lambda: v.memset(o[0], c), [o], [])

    def act(o, i, f, scale=None, bias=None):
        kw = {}
        if scale is not None:
            kw["scale"] = _c(scale)
        if bias is not None:
            kw["bias"] = _c(bias)
        op("s", lambda: sc.activation(o[0], i[0], f, **kw), [o], [i] + _r(scale, bias))

    def mm(items):
        rd = [r for x in items for y in x[1:] for r in y[1]]
        wr = [r for x in items for r in x[0][1]]
        wait("p", need("p", rd, wr))
        n = len(items)
        for j, (o, a, b) in enumerate(items):
            i = g.tensor.matmul(o[0], a[0], b[0], j == 0, j == n - 1)
        cnt["p"] += 1
        i.then_inc(T.sem.p, 1)
        note("p", rd, wr, "p", cnt["p"])

    def dma(e, o, i, sem):
        op(e, lambda: E[e].dma_start(o[0], i[0]), [o], [i], dma=sem)

    def ext(ap, name):
        return (ap, [(name, 0, 1)])

    def arrived(e, name, sem, n):
        if known[e].get(sem, 0) < n:
            E[e].wait_ge(T.sem[sem], n)
            known[e][sem] = n
        total[sem] = n

    def send(dst, buf_src, buf_dst, sem, fwd, loc, which):
        to = _relay(topo, core, dst, which)
        d = dst if to is None else to
        m, n = _mask(topo, core, d)
        rid, pid = topo.addr(d, core)
        name = _ARENA[buf_src][0]
        wait("k", need("k", [(name, 0, 32)], []))
        g.remote_dma(T[buf_dst][:], T[buf_src][:, 0:32], T.sem[sem if to is None else fwd], T.sem[loc], pid, rid, m)
        total[loc] = n

    def landed_n(src, which):
        via = _relay(topo, src, core, which)
        return _mask(topo, src if via is None else via, core)[1]

    def hold(o, z):
        scan(o, u("MS", 0, 128), z, A.mult, A.add)

    def k16(name, k, n=128, p=None):
        return u(name, k, n, 16, p)

    def sums(ps, base, src, w, p=None):
        return [(u(ps, base + k, base + 128, 16, p), u(src, k, None, 16), u(w)) for k in range(16)]

    fill(u("X", 0, 16), 0.0)
    fill(u("X", 2048, 2304), 0.0)
    fill(u("AC4", 0, 8), 0)
    dma("y", u("MI"), ext(T.ml[:], "in_ml"), "ld0")
    op("k", lambda: g.iota(u("PIi", 0, 1)[0], [[0, 1]], 0, 1), [u("PIi", 0, 1)], [])
    op("k", lambda: g.iota(u("J")[0], [[1, 512]], 0, 0), [u("J")], [])
    dma("s", u("X", 1, 2049), ext(T.x0[:], "in_x"), "ld1")
    dma("y", u("LI"), ext(T.lims[:], "in_l"), "ld2")
    dma("s", u("WI"), ext(T.wt[:], "in_w"), "ld3")
    for q in range(4):
        dma("y", u("AC4", 1 + 512 * q, 513 + 512 * q), ext(T.ac[:], "in_a"), "ld%d" % (4 + q))
    op("k", lambda: g.iota(u("J2f")[0], [[1, 128], [0, 4]], 0, 0, allow_small_or_imprecise_dtypes=True), [u("J2f")], [])
    op("k", lambda: g.iota(u("J3")[0], [[0, 128], [1, 4]], 0, 0), [u("J3")], [])
    op("k", lambda: g.iota(u("Jf")[0], [[1, 512]], 1, 0, allow_small_or_imprecise_dtypes=True), [u("Jf")], [])
    op("k", lambda: g.iota(u("OT", 0, 2064)[0], [[0, 2064]], 0, 0, allow_small_or_imprecise_dtypes=True), [u("OT", 0, 2064)], [])
    op("k", lambda: g.iota(u("Z")[0], [[0, 2048]], 0, 0, allow_small_or_imprecise_dtypes=True), [u("Z")], [])

    fill(u("MS"), 1.0)
    fill(u("MS", 0, None, 16), 0.0)
    fill(u("ZE"), 0.0)
    fill(u("MIN"), -BIG)
    fill(u("MIN", 0, None, 16), BIG)
    fill(u("W", 0, 8), 0.0)
    fill(u("W", 512, 664), 0.0)
    J, J4, J15 = u("Jh", 0, 128), u("J4h"), u("J15h")

    def col(n):
        return u("PC", n, n + 1)
    P, P4, P15 = col(0), col(1), col(2)
    ts(u("PIi", 1, 2), u("PIi", 0, 1), 4, A.logical_shift_right)
    ts(u("PIi", 2, 3), u("PIi", 0, 1), 15, A.bitwise_and)
    cp(u("PC", 0, 3), u("PIi", 0, 3))
    ts(u("J4"), u("J", 0, 128), 4, A.logical_shift_right)
    ts(u("J15"), u("J", 0, 128), 15, A.bitwise_and)
    cp(u("Jh"), u("J", 0, 144))
    cp(J4, u("J4"))
    cp(J15, u("J15"))
    ts(col(3), P15, 4, A.is_equal)
    ts(col(4), P15, 4, A.is_equal, 128.0, A.mult)
    ts(col(5), P15, 5, A.is_equal)
    ts(col(27), P15, 5, A.is_equal, 1024.0, A.mult)
    act(u("p4"), u("J2f"), F.Identity, scale=col(3), bias=col(4))
    act(u("p5"), u("Jf"), F.Identity, scale=col(5), bias=col(27))
    ts(u("t512c"), u("J3"), P15, A.is_equal, 64.0, A.mult)
    tt(u("t512c"), u("t512c"), u("p4"), A.add)
    tt(u("V0"), u("t512c"), u("p5"), A.add)
    ts(col(6), P15, 2064, A.add)
    ts(u("DUM"), J, 16, A.mult, col(6), A.add)

    def owners(c):
        a, b = 128 * c, 128 * c + 128
        ve = "VE" if c % 2 == 0 else "VG"
        cp(u("ZE", 0, None, 16), u("V0", a, b))
        scan(u(ve), u("MS"), u("ZE"), A.mult, A.add)
        ts(u("p5", 0, 128), u("MI", a, b), 2048, A.is_equal)
        tt(u("p5", 128, 256), u("DUM"), u("p5", 0, 128), A.mult)
        tt(u("f128a"), u("W", 1 + a, 1 + b), u("p5", 128, 256), A.add)
        cp(u("INO", a, b), u("f128a"))
        act(ix(u("OT"), u("INO", a, b)), u(ve), F.Silu)

    ts(u("p6"), u("MI"), 2048, A.is_lt)
    ts(u("t512c"), u("MI"), 1, A.add)
    tt(u("W", 1, 513), u("t512c"), u("p6"), A.mult)
    owners(0)
    ts(u("IDB"), J, P, A.is_equal)
    ts(u("NIDB"), J, P, A.is_equal, -1.0, A.mult)
    ts(u("ID16"), J, P, A.is_equal)
    ts(u("NID16"), J, P, A.is_equal, -1.0, A.mult)
    ts(u("ID16x"), J, P, A.is_equal, 16.0, A.mult)
    ts(u("IDE"), J, P, A.is_equal, 2.0 ** 23, A.mult)
    ts(u("NIDE"), J, P, A.is_equal, -2.0 ** 23, A.mult)
    ts(u("ID1K"), J, P, A.is_equal, 1024.0, A.mult)
    ts(u("BD"), J4, P4, A.is_equal)
    ts(u("NBD"), J4, P4, A.is_equal, -1.0, A.mult)
    ts(u("R16"), J15, P15, A.is_equal)
    ts(u("p3", 0, 128), J15, P15, A.is_equal)
    ts(u("CK"), J15, 2048.0, A.mult)
    ts(u("CKP"), J15, 1.0, A.add)
    ts(u("blk16"), u("J", 0, 8), P4, A.is_equal)
    ts(u("blkf"), u("J", 0, 8), P4, A.is_equal)
    ts(u("w32k"), u("BD", 0, None, 16), 32768.0, A.mult)
    ts(u("w8k"), u("BD", 0, None, 16), 8192.0, A.mult)
    ts(u("w2k"), u("BD", 0, None, 16), 2048.0, A.mult)
    ts(u("w512"), u("BD", 0, None, 16), 512.0, A.mult)
    ts(u("w1"), u("BD", 0, None, 16), 1.0, A.mult)
    ts(u("w2"), u("BD", 0, None, 16), 2.0, A.mult)
    owners(1)
    for z in "ZS ZD ZN ZBB ZM ZW ZSP ZI ZV ZQ".split():
        ts(u(z), J, 0.0, A.mult)

    def late_constants():
        ts(col(7), P, -16.0, A.mult, 2047.0, A.add)
        ts(u("KB"), J15, -1.0, A.mult, col(7), A.add)
        ts(col(8), P, 16.0, A.mult)
        ts(u("KV"), J15, col(8), A.add)
        cp(u("CREP"), J)
        ts(col(9), P, 0.0, A.is_equal, 512.0, A.mult)
        ts(col(10), P, 1.0, A.is_equal, -2.0 ** 24, A.mult)
        ts(u("KA"), J15, col(9), A.mult, col(10), A.add)
        fill(u("ONEB"), 1.0)
        cp(u("ONE16"), u("ONEB"))
        ts(col(11), P15, 0.0, A.is_equal, 2.0 ** 25, A.mult)
        ts(u("DEAD"), u("BD"), col(11), A.mult)
        ts(col(12), P15, 4.0, A.is_lt, 1.0 / 64, A.mult)
        tt(col(12), col(12), P15, A.mult)
        ts(col(13), P15, 4.0, A.is_equal, 4.0, A.mult)
        tt(col(12), col(12), col(13), A.add)
        ts(u("HWB"), u("BD"), col(12), A.mult)
        for c in range(4):
            ts(col(14), P15, float(c), A.is_equal, 2.0 ** 19, A.mult)
            tt(col(15), col(14), col(12), A.add)
            ts(u("og%d" % c), u("BD", 0, None, 16), col(15), A.mult)
        ts(u("TRI"), J, P, A.is_gt)
        fill(u("FM"), -4096.0)
        fill(u("FM", 0, None, 128), 4096.0)
        ts(u("blk128"), u("J", 0, 8), P4, A.is_equal, 128.0, A.mult)
        ts(col(16), P, -1.0, A.mult, -528.0, A.add)
        ts(u("blkN"), u("J", 0, 8), P4, A.is_equal, col(16), A.mult)
        ts(col(28), P, -1.0, A.mult, -1552.0, A.add)
        ts(u("blkE"), u("J", 0, 8), P4, A.is_equal, col(28), A.mult)
        ts(col(17), P, 16.0, A.add)
        ts(u("blkI"), u("J", 0, 8), P4, A.is_equal, col(17), A.mult)
        ts(col(18), P, 32.0, A.add)
        ts(u("blk32"), u("J", 0, 8), P4, A.is_equal, col(18), A.mult)
        ts(u("blkm"), u("J", 0, 8), P4, A.is_equal, -640.0, A.mult)
        ts(u("blk2k"), u("J", 0, 8), P4, A.is_equal, 2048.0, A.mult)
        fill(u("C640"), 640.0)
        ts(u("CI"), u("J", 0, 8), 16.0, A.mult, P15, A.add)
        ts(col(19), P15, 528.0, A.add)
        ts(u("C528"), u("J", 0, 8), 16.0, A.mult, col(19), A.add)
        ts(u("SEL5"), u("BD"), col(5), A.mult)
        ts(u("BT"), J, P, A.is_le, -1.0, A.mult)
        tt(u("BT"), u("BT"), u("BD"), A.mult)
        ts(col(20), P, 15.0, A.add)
        ts(col(21), P15, 0.0, A.is_equal)
        ts(u("Y"), u("J", 0, 144), col(20), A.is_equal, col(21), A.mult)
        ts(u("SEL0"), u("BD", 0, None, 16), col(21), A.mult)
        ts(col(22), P15, 656.0, A.add)
        ts(u("CVp"), u("J", 0, 32), 16.0, A.mult, col(22), A.add)
        ts(u("CVn"), u("CVp"), -1.0, A.mult)
        fill(u("FREE"), 0.0)
        fill(u("STI", 0, 8), 0)
        fill(u("DS", 2048, 2176), 0.0)
        fill(u("RESW"), 0)
        fill(u("QZ"), 0.0)
        fill(u("Aa"), 0)
        for t in range(RO):
            fill(u("XV%d" % t), 0.0)
        for s in range(16):
            o, i = u("SH", 128 * s, 128 * s + 128), u("BD")
            op("k", lambda: g.affine_select(o[0], i[0], [[1, 128]], A.is_equal, 0.0, -s, -1), [o], [i])
        cp(u("PC", 24, 26), u("LI"))
        cp(u("PC", 26, 27), u("WI"))
        ts(u("WTB"), u("BD"), col(26), A.mult)
        ts(u("NFH"), u("SEL0"), col(24), A.mult)
        mm([(u("p6", 0, 8), u("ONE16"), u("NFH"))])
        cp(u("lim8"), u("p6", 0, 8))
        cp(u("thr8"), u("p6", 0, 8))
        ts(u("NFH"), u("SEL0"), col(25), A.mult)
        mm([(u("p6", 0, 8), u("ONE16"), u("NFH"))])
        cp(u("lim28"), u("p6", 0, 8))

    def tile(src_rep, prod, blk, out, extra=(), ps="p6"):
        if src_rep is not None:
            tt(u(prod), src_rep, u("p3", 0, 128), A.mult)
        mm([(u(ps, 0, 8), u(prod), u(blk))] + [(u(ps, 0, 8), u(a), u(b)) for a, b in extra])
        cp(u(out), u(ps, 0, 8))

    def part_own(t):
        cl = t % 4
        lanes = u("W", 1 + cl, 513, 4)
        cp(u("OWN"), lanes)
        win = u("X", 0, 2064)
        if t == 0:
            cp(u("T"), ix(win, u("OWN")))
        else:
            act(u("T", 1024, 2048), ix(win, u("OWN", 64, 128)), F.Copy)
            cp(u("T", 0, 1024), ix(win, u("OWN", 0, 64)))
        ts(u("EO"), lanes, 0.0, A.is_equal)
        cp(u("OWNH"), lanes)
        ts(u("VC"), u("W", 1, 513), 0.0, A.is_equal)
        mm([(u("p4", 0, 128), u("IDB"), u("CK")), (u("p4", 0, 128), u("EO"), u("IDE")), (u("p4", 0, 128), u("OWNH"), u("ID16"))]
           + sums("p4", 0, "T", "w32k"))
        scan(u("US"), u("MS", 0, 2048), u("T"), A.mult, A.max)
        mm([(u("p7", 32, 40), u("EO"), u("BD", 0, None, 16))])
        mm([(u("p5", 128, 256), u("OWNH"), u("ID16x"))])
        mm([(u("p5", 256, 384), u("OWNH"), u("ID16x")), (u("p5", 256, 384), u("IDB"), u("CKP"))])
        mm([(u("p6", 8, 16), u("US", 15, None, 16), u("BD", 0, None, 16))])
        scan(u("S1"), u("MIN"), u("p4", 0, 128), A.max, A.min)
        ts(u("k8"), u("S1", 15, None, 16), -1.0, A.add)
        ts(u("sv8"), u("k8"), 2047, A.bitwise_and)
        ts(u("sx8"), u("k8"), 15, A.logical_shift_right)
        ts(u("ZS", 0, None, 16), u("sv8"), 1.0, A.add)
        ts(u("live8"), u("S1", 15, None, 16), 2.0 ** 23, A.is_lt)
        hold(u("SR"), u("ZS"))
        tile(u("SR"), "PS", "blk16", "S16")
        cp(u("Z", 0, None, 16), ix(win, u("S16")))
        mm([(u("p7", 0, 32), u("Y", 15 - r, 143 - r), u("VC", r, None, 16)) for r in range(16)] if t else
           [(u("p7", 0, 32), u("IDB"), u("VC", 0, 32))])
        ts(u("ZN", 0, None, 16), u("p7", 32, 40), -1.0, A.mult, 16.0, A.add)
        tt(u("gr8"), u("p6", 8, 16), u("sx8"), A.subtract)
        scan(u("REP"), u("MS", 0, 2048), u("Z"), A.mult, A.add)

    def dif(c):
        a, b = 512 * c, 512 * c + 512
        ps = "p%d" % (c % 3)
        mm([(u(ps), u("IDB"), u("T", a, b)), (u(ps), u("NIDB"), u("REP", a, b))])
        act(u("SQ", a, b), u(ps), F.Square)

    def part_own_squares(t):
        for c in (2, 3):
            dif(c)
        act(u("SQS"), u("Z", 0, None, 16), F.Square)
        act(u("W16L"), u("p5", 128, 256), F.Copy)
        act(u("WL"), u("p5", 128, 256), F.Copy, scale=0.0625)
        act(u("PW2"), u("p5", 256, 384), F.Copy)

    def part_own_end(t):
        tt(u("gr8"), u("gr8"), u("lim28"), A.is_gt)
        tt(u("wp8"), u("gr8"), u("live8"), A.mult)

    def part_sizes(t):
        hold(u("NR"), u("ZN"))
        tt(u("NP"), u("NR"), u("p3", 0, 128), A.mult)
        mm([(u("p4", 264, 272), u("NP"), u("blk128")), (u("p4", 264, 272), u("ID16"), u("CI"))])

    def part_split(t):
        cp(u("N16"), u("p4", 264, 272))
        cp(u("nf8"), u("p4", 256, 264))
        mm([(u("p5", 0, 128), u("ID16"), u("KB")), (u("p5", 0, 128), u("EO"), u("NIDE"))] + sums("p5", 0, "SQ", "w2k"))
        scan(u("SB"), u("MS", 0, 128), u("p5", 0, 128), A.mult, A.max)
        cp(u("b8"), u("SB", 15, None, 16))
        ts(u("bb8"), u("b8"), 2047, A.bitwise_and)
        ts(u("ZBB", 0, None, 16), u("bb8"), -1.0, A.mult, 2047.0, A.add)
        hold(u("BR"), u("ZBB"))
        tile(u("BR"), "BP", "blk16", "B16", ps="p7")
        cp(u("XB"), ix(u("T"), u("B16")))
        act(u("SQB"), u("XB"), F.Square)
        tt(u("WV"), u("Z", 0, None, 16), u("XB"), A.subtract)
        tt(u("AX"), ix(u("WV"), u("CREP")), u("T"), A.mult)
        mm([(u("p5", 384, 512), u("SQB"), u("BD")), (u("p5", 384, 512), u("SQS"), u("NBD"))] + sums("p5", 384, "AX", "w2"))

    def part_compact(t):
        ts(u("mb"), u("W16L"), 0.0, A.is_gt)
        ts(u("p5", 0, 128), u("p5", 384, 512), 0.0, A.is_lt)
        tt(u("L1"), u("mb"), u("p5", 0, 128), A.mult)
        scan(u("p5", 128, 256), u("MS", 0, 128), u("L1"), A.mult, A.add)
        tt(u("SM"), u("mb"), u("L1"), A.subtract)
        tt(u("p5", 0, 128), u("PW2"), u("p5", 128, 256), A.subtract)
        tt(u("p5", 256, 384), u("W16L"), u("p5", 128, 256), A.add)
        tt(u("Pa", 128, 256), u("L1"), u("p5", 0, 128), A.mult)
        tt(u("Pa", 0, 128), u("SM"), u("p5", 256, 384), A.mult)

    def part_shift(t, steps):
        for s in steps:
            a, b = ("Pa", "Pb") if s % 2 == 0 else ("Pb", "Pa")
            ts(u("Mi", 0, 256), u(a, 0, 256), 1 << s, A.bitwise_and)
            ts(u("p5", 0, 256), u("Mi", 0, 256), 2.0 ** (16 - s), A.mult)
            tt(u("p5", 256, 512), u(a, 0, 256), u("p5", 0, 256), A.subtract)
            tt(u("Aa", 0, 256), u(a, 0, 256), u("p5", 0, 256), A.min)
            tt(u(b, 0, 256), u("p5", 256, 512), u("Aa", 1 << s, 256 + (1 << s)), A.max)
        if 3 in steps:
            ts(u("STI"), u("Pa", 0, 256), 4, A.logical_shift_right)
            tt(u("STM"), u("STI", 0, 128), u("WL"), A.subtract)

    def move_owners():
        act(ix(u("OT", 0, 4112), u("MVO")), u("VE"), F.Silu)

    def part_vacant_count(t):
        if t == 0:
            mm([(u("p7", 0, 32), u("Y", 15 - r, 143 - r), u("VC", r, None, 16)) for r in range(16)])
        cp(u("VTb"), u("p7", 0, 32))
        mm([(u("p7", 0, 32), u("BD"), u("VTb"))])
        mm([(u("p6", 0, 32), u("BT"), u("VTb")), (u("p6", 0, 32), u("ID16"), u("CVn"))])
        part_sizes(t)

    def part_vacant(t):
        scan(u("CSs"), u("ONEB", 0, 32), u("p7", 0, 32), A.mult, A.add)
        tt(u("rk"), u("CSs"), u("p6", 0, 32), A.add)
        tt(u("rk"), u("rk"), u("VTb"), A.mult)
        tt(u("rk"), u("rk"), u("CVp"), A.add)
        cp(u("F16"), u("rk"))
        ts(u("NFH"), u("SEL0"), u("CSs", 31, 32), A.mult)
        mm([(u("p4", 256, 264), u("ONE16"), u("NFH"))])

    def part_near(t):
        cl = t % 4
        win = u("X", 0, 2064)
        i = ix(u("AC4"), u("S16"))
        ts(u("AN"), i, 1, A.add)
        act(u("OG"), ix(u("OT", 0, 2064), u("AN")), F.Copy)

    def part_distances(t):
        cl = t % 4
        win = u("X", 0, 2064)
        for h in range(2):
            a, b = 1024 * h, 1024 * h + 1024
            tt(u("AX", a, b), ix(win, u("AN", 64 * h, 64 * h + 64)), u("REP", a, b), A.subtract)
            act(u("SQ", a, b), u("AX", a, b), F.Square)
        mm([(u("p4", 0, 128), u("ONEB"), u("KA")), (u("p4", 0, 128), u("EO"), u("DEAD"))] + sums("p4", 0, "OG", "og%d" % cl)
           + sums("p4", 0, "SQ", "w8k"))

    def part_partner(t):
        win = u("X", 0, 2064)
        scan(u("S2"), u("MIN"), u("p4", 0, 128), A.max, A.min)
        cp(u("a8"), u("S2", 15, None, 16))
        ts(u("has8"), u("S2", 15, None, 16), 14.0e6, A.is_lt)
        ts(u("d8"), u("a8"), 511, A.bitwise_and)
        ts(u("dp8"), u("d8"), 1.0, A.add)
        tt(u("ZD", 0, None, 16), u("dp8"), u("has8"), A.mult)
        hold(u("D1R"), u("ZD"))
        tile(u("D1R"), "PD", "blk16", "D16")
        lists = ix(u("W", 0, 520), u("D16"))
        cp(u("DM"), lists)
        act(u("DT", 1024, 2048), ix(win, u("DM", 64, 128)), F.Copy)
        cp(u("DT", 0, 1024), ix(win, u("DM", 0, 64)))
        cp(u("DMH"), ix(u("W", 0, 520), u("D16")))
        ts(u("ED"), u("DM"), 0.0, A.is_equal)
        ts(u("nD"), u("ZD", 0, None, 16), -1.0, A.mult)
        tt(u("d18"), u("dp8"), u("has8"), A.mult)
        for q in range(8):
            ts(u("DG", 128 * q, 128 * q + 128), u("ID16"), u("d18", q, q + 1), A.mult)
        for q in range(8):
            ps = "p%d" % (q // 4)
            lo = 128 * (q % 4)
            mm([(u(ps, lo, lo + 128), u("TRI"), u("DG", 128 * q, 128 * q + 128))])
        mm([(u("p7", 0, 8), u("EO"), u("BD", 0, None, 16)), (u("p7", 0, 8), u("ED"), u("BD", 0, None, 16))])
        mm([(u("p4", 0, 128), u("ED"), u("ID1K"))] + sums("p4", 0, "DT", "w1"))
        scan(u("AX"), u("MS", 0, 2048), u("DT"), A.mult, A.max)
        tt(u("Vv"), u("US", 15, None, 16), u("AX", 15, None, 16), A.max)
        mm([(u("p6", 0, 8), u("Vv"), u("BD", 0, None, 16))])
        for q in range(8):
            ps = "p%d" % (q // 4)
            lo = 128 * (q % 4)
            act(u("AB", 128 * q, 128 * q + 128), u(ps, lo, lo + 128), F.Abs, bias=u("nD", q, q + 1))
        for c in range(4):
            ps = "p%d" % (2 - 2 * (c % 2))
            for k in range(4):
                s = 4 * c + k
                mm([(u(ps, 128 * k, 128 * k + 128), u("SH", 128 * s, 128 * s + 128), u("DMH"))])
            act(u("DS", 512 * c, 512 * c + 512), u(ps), F.Copy)
        act(ix(u("FREE"), u("F16")), u("V0"), F.Silu)
        ts(u("sz8"), u("p7", 0, 8), 16.0, A.is_ge)
        scan(u("S3"), u("MIN"), u("p4", 0, 128), A.max, A.min)
        tt(u("mn8"), u("S3", 15, None, 16), u("sx8"), A.min)
        tt(u("tm8"), u("mn8"), u("thr8"), A.add)
        scan(u("ABS"), u("FM"), u("AB"), A.max, A.min)
        ts(u("f8"), u("ABS", 127, None, 128), 0.5, A.is_ge)
        tt(u("P0"), u("f8"), u("has8"), A.mult)
        tt(u("P0"), u("P0"), u("sz8"), A.mult)

    def part_finish(t):
        cl = t % 4
        zm, zw, zs, zi, zv = [u(z, 0, None, 16) for z in ("ZM", "ZW", "ZSP", "ZI", "ZV")]
        tt(u("c8"), u("p6", 0, 8), u("tm8"), A.is_le)
        tt(zm, u("c8"), u("P0"), A.mult)
        tt(zw, u("wp8"), zm, A.is_gt)
        hold(u("WR"), u("ZW"))
        mm([(u("p7", 0, 128), u("TRI"), u("WR"))])
        hold(u("MR"), u("ZM"))
        mm([(u("p4", 0, 128), u("MR"), u("ID16"))])
        tt(u("sp8"), u("p7", 0, 128, 16), u("nf8"), A.is_lt)
        tt(zs, u("sp8"), zw, A.mult)
        tt(u("ms8"), zm, zs, A.add)
        tt(zi, u("live8"), u("ms8"), A.is_gt)
        hold(u("IR"), u("ZI"))
        mm([(u("p6", 128, 256), u("TRI"), u("IR"))])
        hold(u("p3", 128, 256), u("ZSP"))
        tt(u("SPP"), u("R16"), u("p3", 128, 256), A.mult)
        tt(u("KP"), u("p7", 0, 128), u("SPP"), A.mult)
        ts(u("v8"), u("p6", 128, 256, 16), 32.0, A.is_lt)
        tt(zv, u("v8"), zi, A.mult)
        hold(u("p3", 256, 384), u("ZV"))
        tt(u("VP"), u("R16"), u("p3", 256, 384), A.mult)
        tt(u("RP"), u("p6", 128, 256), u("VP"), A.mult)
        tt(u("NVP"), u("p3", 0, 128), u("VP"), A.subtract)
        tile(None, "RP", "blk16", "RT16", [("NVP", "blk32")])
        xv = "XV%d" % t
        cp(ix(u(xv), u("RT16")), u("Z", 0, None, 16))
        send(T.cores[(rank + 1 + t % 7) % 8], xv, "QI%d" % t, "rq%d" % t, "fq%d" % t, "lq%d" % t, 0)
        tile(None, "KP", "blk16", "K16", [("SPP", "blkm"), ("IDB", "C640")], ps="p7")
        cp(u("EV"), ix(u("FREE"), u("K16")))
        cp(u("EVH"), u("EV"))
        mm([(u("p7", 0, 128), u("EVH"), u("SEL5"))])
        tt(u("f128a"), u("p4", 0, 128), u("V0", cl, None, 4), A.mult)
        tt(u("VF"), u("f128a"), u("EV"), A.add)
        act(u("VE"), ix(u("VF"), u("CREP")), F.Copy)
        tt(u("A3"), u("STI", 128, 256), u("p3", 128, 256), A.mult)
        mm([(u("p5", 128, 256), u("A3"), u("ID16"))])
        tt(u("MD"), u("p4", 0, 128), u("DMH"), A.mult)
        mm([(u("p2", 0, 128), u("ID16"), u("MD")), (u("p2", 0, 128), u("A3"), u("ID16"))])
        cp(u("DSE"), ix(u("DS"), u("N16")))
        tt(u("A1"), u("p4", 0, 128), u("DSE"), A.mult)
        tt(u("A2"), u("STM"), u("p3", 128, 256), A.mult)
        mm([(u("p5", 0, 128), u("ID16"), u("OWNH")), (u("p5", 0, 128), u("ID16"), u("A1")), (u("p5", 0, 128), u("A2"), u("ID16"))])
        ts(u("p3", 384, 512), u("p2", 0, 128), 0.0, A.is_equal)
        tt(u("f128b"), u("DUM"), u("p3", 384, 512), A.mult)
        tt(u("f128b"), u("f128b"), u("p2", 0, 128), A.add)
        cp(u("MVO"), u("f128b"))
        tt(u("MP"), u("MR"), u("p3", 0, 128), A.mult)
        tt(u("Q1"), u("PD"), u("MR"), A.mult)
        tt(u("Q2"), u("p7", 0, 128), u("SPP"), A.mult)
        cp(u("ELS"), u("p5", 128, 256))
        tile(None, "Q1", "blk16", "TG16", [("Q2", "blk16"), ("MP", "blkN"), ("SPP", "blkE"), ("ID16", "C528")])
        cp(u("W", 1 + cl, 513, 4), u("p5", 0, 128))
        cp(ix(u("W", 0, 656), u("TG16")), u("ELS"))

    def part_late(t):
        tt(u("XP"), u("PS"), u("p3", 256, 384), A.mult)
        tile(None, "XP", "blk16", "XT16", [("NVP", "blkI"), ("NVP", "blk2k")])
        if t + 1 < RO:
            mm([(u("p7", 0, 8), u("ONE16"), u("MR", 0, None, 16))])
            op("v", lambda: v.tensor_reduce(u("mc", 0, 1)[0], u("p7", 0, 8)[0], AX_.X, A.add), [u("mc", 0, 1)], [u("p7", 0, 8)])
            cp(u("mci", 0, 1), u("mc", 0, 1))
            ts(u("mci", 1, 2), u("mci", 0, 1), 15, A.bitwise_and)
            cp(u("mc", 1, 2), u("mci", 1, 2))
            ts(u("thr8"), u("lim8"), u("mc", 1, 2), A.add)

    def part_serve(t):
        src = T.cores[(rank - 1 - t % 7) % 8]
        n = landed_n(src, 0)
        qi, sn = "QI%d" % t, "SN%d" % t
        rq = "rq%d" % t
        p32 = (0, 32)
        for e in ("p", "v"):
            arrived(e, qi, rq, n)
        mm([(u("p6", 0, 128, 1, p32), u(qi), u("WTB"))])
        cp(u("QZ", 0, None, 16), u(qi))
        tt(u("VFP", p=p32), u("p6", 0, 128, 1, p32), u("R16", p=p32), A.mult)
        mm([(u("p7", 0, 2), u("VFP", p=p32), u("blkf", 0, 2, 1, p32))])
        cp(u("VI"), u("p7", 0, 2))
        ts(u("VI2"), u("VI"), 2047, A.bitwise_and)
        ts(u("VV16"), u("VI2"), 1, A.add)
        scan(u("QRp"), u("MS", 0, 512), u("QZ"), A.mult, A.add)
        cp(u("HO"), ix(u("OT", 0, 2064), u("VV16")))
        mm([(u("p6", 0, 128, 1, p32), u("HO"), u("HWB"))])
        tt(u("QP", p=p32), u("p6", 0, 128, 1, p32), u("R16", p=p32), A.mult)
        mm([(u("p7", 0, 2), u("QP", p=p32), u("blk16", 0, 2, 1, p32))])
        ts(u("H16"), u("p7", 0, 2), -511.0, A.add)
        cp(u("HL"), ix(u("W", 0, 520), u("H16")))
        tt(u("QD"), ix(u("X", 0, 2064), u("HL")), u("QRp"), A.subtract)
        ts(u("EH"), u("HL"), 0.0, A.is_equal)
        act(u("QS"), u("QD"), F.Square)

    def part_serve_met(t):
        src = T.cores[(rank - 1 - t % 7) % 8]
        qi, sn = "QI%d" % t, "SN%d" % t
        p32 = (0, 32)
        mm([(u("p6", 0, 128, 1, p32), u("ID16", 0, 32), u("KV")), (u("p6", 0, 128, 1, p32), u("EH"), u("IDE"))]
           + sums("p6", 0, "QS", "w512", p32))
        scan(u("QSC", p=p32), u("MIN", p=p32), u("p6", 0, 128, 1, p32), A.max, A.min)
        cp(u("q8", p=p32), u("QSC", 15, None, 16, p32))
        ts(u("qq8", p=p32), u("q8", p=p32), 511, A.bitwise_and)
        cp(u("ZQ", 0, None, 16, p32), u("qq8", p=p32))
        scan(u("QR8", p=p32), u("MS", 0, 128, 1, p32), u("ZQ", p=p32), A.mult, A.add)
        tt(u("QP", p=p32), u("QR8", p=p32), u("R16", p=p32), A.mult)
        mm([(u("p7", 0, 2), u("QP", p=p32), u("blk16", 0, 2, 1, p32))])
        cp(u("J16"), u("p7", 0, 2))
        ts(u("hs"), ix(u("QD"), u("J16")), -0.5, A.add, 0.5, A.mult)
        tt(u(sn), u("hs"), u(qi), A.add)
        send(src, sn, "RS%d" % t, "rs%d" % t, "fs%d" % t, "ls%d" % t, 1)

    def part_apply(t):
        src = T.cores[(rank + 1 + t % 7) % 8]
        arrived("v", "RS%d" % t, "rs%d" % t, landed_n(src, 1))
        cp(u("RESW", 0, 32), u("RS%d" % t))
        cp(u("NV"), ix(u("RESW"), u("RT16")))
        cp(ix(u("X"), u("XT16")), u("NV"))

    part_own(0)
    dif(0)
    dif(1)
    part_own_squares(0)
    owners(2)
    late_constants()
    part_own_end(0)
    owners(3)
    part_vacant_count(0)
    part_vacant(0)
    part_split(0)
    for t in range(RO):
        part_near(t)
        part_compact(t)
        part_shift(t, (0, 1))
        if t:
            part_apply(t - 1)
        part_distances(t)
        part_shift(t, (2, 3))
        part_partner(t)
        part_finish(t)
        part_late(t)
        if t + 1 < RO:
            part_own(t + 1)
            move_owners()
            part_vacant_count(t + 1)
            dif(0)
            dif(1)
            part_own_end(t + 1)
            part_vacant(t + 1)
            part_serve(t)
            part_own_squares(t + 1)
            part_serve_met(t)
            part_split(t + 1)
        else:
            move_owners()
            ts(u("t512a"), u("W", 1, 513), 0.0, A.is_equal, 2049.0, A.mult)
            ts(u("t512b"), u("W", 1, 513), -1.0, A.add)
            tt(u("YM"), u("t512a"), u("t512b"), A.add)
            dma("y", ext(T.ym[:], "out_m"), u("YM"), "st0")
            part_serve(t)
            part_serve_met(t)
            part_apply(t)
            dma("y", ext(T.yx[:], "out_x"), u("X", 1, 2049), "st1")
    for sem in total:
        n = total[sem]
        if known["k"].get(sem, 0) < n:
            g.wait_ge(T.sem[sem], n)
